import numpy as np
import ml_dtypes


def mxq(x, axis, fmt="e4m3"):
    dtype, down = {"e4m3": (ml_dtypes.float8_e4m3fn, 7), "e5m2": (ml_dtypes.float8_e5m2, 14)}[fmt]
    v = np.moveaxis(np.asarray(x, np.float32).astype(ml_dtypes.bfloat16).astype(np.float64), axis, -1)
    blocks = v.reshape(v.shape[:-1] + (-1, 32))
    amax = np.abs(blocks).max(-1, keepdims=True)
    byte = np.maximum(np.where(amax > 0, np.frexp(amax)[1] - 1 + 127, 0) - down, 1)
    scale = np.exp2(byte - 127.0)
    codes = (blocks / scale).astype(np.float32).astype(dtype).astype(np.float64)
    return np.moveaxis((codes * scale).reshape(v.shape), -1, axis)


WIDE = False


def mx_kscale(k):
    if not WIDE:
        return np.ones(k)
    levels = np.array([10, -10, 5, -5, 0])
    if k % 512:
        return np.exp2(np.random.permutation(np.resize(levels, k // 32))).repeat(32)
    a = np.empty((k // 512, 16))
    for p in range(k // 512):
        a[p, :8] = np.random.permutation(np.resize(levels, 8))
        for g in range(8):
            far = levels[np.abs(levels - a[p, g]) >= 10]
            a[p, g + 8] = far[np.random.randint(len(far))]
    return np.exp2(a.ravel()).repeat(32)


def f64(x):
    return np.asarray(x).astype(np.float64)


def striped(idx):
    return np.tile(idx.reshape(-1, 16).T, (8, 1)).astype(np.uint16)


def unstriped(offs):
    return offs[:16].T.reshape(-1).astype(np.int64)


def pack_weight(w):
    k, n = w.shape
    w = f64(np.asarray(w, np.float32).astype(ml_dtypes.bfloat16)).reshape(k // 32, 32, n)
    amax = np.abs(w).max(1)
    byte = np.clip(np.where(amax > 0, np.frexp(amax)[1] - 1 + 127 - 7, 1), 1, 254)
    scaled = (w * np.exp2(127.0 - byte)[:, None, :]).reshape(k, n).astype(np.float32)
    words = np.ascontiguousarray(scaled.reshape(k // 512, 128, 4, n).transpose(0, 1, 3, 2)).astype(ml_dtypes.float8_e4m3fn).view(np.uint8)
    return words, np.ascontiguousarray(byte.astype(np.uint8).reshape(k // 512, 16, n))


def unpack_weight(words, scales):
    g, p, n, _ = words.shape
    vals = np.ascontiguousarray(words).view(ml_dtypes.float8_e4m3fn).astype(np.float64) * np.repeat(np.exp2(scales.astype(np.float64) - 127.0), 8, axis=1)[..., None]
    return vals.transpose(0, 1, 3, 2).reshape(g * 512, n)


def gelu(v):
    return 0.5 * v * (1.0 + np.tanh(np.sqrt(2.0 / np.pi) * (v + 0.044715 * v**3)))


K, T, S, N, U = 512, 1024, 512, 128, 1024
P = 2 ** 7


def setup_inputs():
    n = np.random.standard_normal
    s = mx_kscale(K)[:, None]
    packed_w1 = pack_weight(n((K, N)) / np.sqrt(K) / s)
    return {
        "xT": (n((K, T)) * s).astype(np.float32),
        "gate": np.tile(np.random.uniform(0.5, 1.5, S), (P, 1)).astype(np.float32),
        "w1_words": packed_w1[0],
        "w1_scales": packed_w1[1],
        "offs": striped(np.random.permutation(T)[:S]),
        "dst": striped(np.random.permutation(U)[:S]),
    }


def reference(xT, gate, w1_words, w1_scales, offs, dst):
    xq = mxq(f64(xT)[:, unstriped(offs)], 0, "e4m3")
    y = gelu(unpack_weight(w1_words, w1_scales).T @ xq)
    out = np.zeros((N, U))
    out[:, unstriped(dst)] = y * f64(gate)[:1]
    return out

@@ -1,0 +1,119 @@
+from contextlib import ExitStack
+
+import concourse.mybir as mybir
+
+F32 = mybir.dt.float32
+BF16 = mybir.dt.bfloat16
+I32 = mybir.dt.int32
+U32 = mybir.dt.uint32
+U16 = mybir.dt.uint16
+U8 = mybir.dt.uint8
+FP8X4 = mybir.dt.float8_e4m3fn_x4
+GELU = mybir.ActivationFunctionType.Gelu_apprx_tanh
+COPY = mybir.ActivationFunctionType.Copy
+MULT = mybir.AluOpType.mult
+
+P = 128
+PACK = 4
+K, T, S, N, U = 512, 1024, 512, 128, 1024
+CH = 128
+NCH = S // CH
+LC = CH // 16
+FLOPS = 2 * K * S * N
+
+
+def tile_picked_route2_lingelu_e_kernel(tc, xT, gate, w1_words, w1_scales, offs, dst, out):
+    nc = tc.nc
+    with ExitStack() as ctx:
+        keep = ctx.enter_context(tc.tile_pool(name="keep", bufs=1))
+        psum = ctx.enter_context(tc.psum_pool(name="psum", bufs=1))
+
+        offs_sb = keep.tile([P, S // 16], U16, name="offs_sb")
+        dst_sb = keep.tile([P, S // 16], U16, name="dst_sb")
+        planes = [keep.tile([P, T], F32, name=f"plane{j}") for j in range(PACK)]
+        w_codes = keep.tile([P, N], U32, name="w_codes", align_bytes=64)
+        w_scale = keep.tile([P, N], U8, name="w_scale", align_bytes=64)
+        gate_sb = keep.tile([P, S], F32, name="gate_sb")
+        window = keep.tile([P, U], F32, name="window")
+        zero = keep.tile([P, 1], F32, name="zero")
+        bias = keep.tile([P, 1], F32, name="bias")
+
+        nc.vector.memset(w_scale[:].bitcast(I32), 0)
+        nc.vector.memset(zero[:], 0.0)
+        nc.vector.memset(window[:], 0.0)
+        nc.scalar.activation(bias[:], zero[:], GELU)
+
+        x_rows = xT.rearrange("(p j) t -> p j t", j=PACK)
+        nc.sync.dma_start(offs_sb[:], offs)
+        for j in range(PACK):
+            nc.sync.dma_start(planes[j][:], x_rows[:, j, :])
+            if j == 0:
+                nc.sync.dma_start(dst_sb[:], dst)
+        nc.scalar.dma_start(w_codes[:].bitcast(I32), w1_words[0].rearrange("p n t -> p (n t)").bitcast(I32))
+        for q in range(4):
+            nc.scalar.dma_start(w_scale[32 * q : 32 * q + 4, :].bitcast(I32), w1_scales[0, 4 * q : 4 * q + 4, :].bitcast(I32))
+        nc.sync.dma_start(gate_sb[:], gate)
+
+        rest = S - CH
+        staging = keep.tile([P, PACK * rest - 2 * CH + PACK * CH], BF16, name="staging", align_bytes=64)
+        picked = staging[:, : PACK * rest].rearrange("p (j s) -> p j s", j=PACK)
+        woven = [staging[:, PACK * rest - 2 * CH :].rearrange("p (s j) -> p s j", j=PACK)]
+        woven += [keep.tile([P, CH, PACK], BF16, name=f"woven{c}", align_bytes=64)[:] for c in range(1, NCH - 1)]
+        rounded = keep.tile([P, T], BF16, name="rounded")
+        codes = [keep.tile([P, CH], U32, name=f"codes{c}", tag=f"codes{c}", align_bytes=64) for c in range(NCH)]
+        scales = [keep.tile([P, CH], U8, name=f"scales{c}", align_bytes=64) for c in range(NCH)]
+        acc = [psum.tile([P, CH], F32, name=f"acc{c}") for c in range(NCH)]
+        y = [keep.tile([P, CH], F32, name=f"y{c}") for c in range(NCH)]
+
+        def gather(j, c0, c1):
+            target = woven[0][:, :, j] if c0 == 0 else picked[:, j, (c0 - 1) * CH : (c1 - 1) * CH]
+            nc.vector.tensor_copy(target, planes[j][:].indirect(offs_sb[:, c0 * LC : c1 * LC]))
+
+        def weave(c):
+            if c == NCH - 1:
+                woven.append(keep.tile([P, CH, PACK], BF16, name=f"woven{c}", tag="codes1", align_bytes=64)[:])
+            nc.scalar.copy(
+                woven[c].rearrange("p (g i) j -> p g j i", i=4),
+                picked[:, :, (c - 1) * CH : c * CH].rearrange("p j (g i) -> p g j i", i=4),
+            )
+
+        def product(c):
+            nc.vector.quantize_mx(out=codes[c][:].bitcast(FP8X4), scales=scales[c][:], in_=woven[c].rearrange("p s j -> p (s j)"))
+            nc.tensor.matmul_mx(
+                out=acc[c][:],
+                lhsT=w_codes[:].bitcast(FP8X4),
+                lhsT_scale=w_scale[:],
+                rhs=codes[c][:].bitcast(FP8X4),
+                rhs_scale=scales[c][:],
+                start=True,
+                stop=True,
+            )
+
+        def activate(c):
+            nc.scalar.activation(y[c][:], acc[c][:], GELU, bias=bias[:])
+
+        def scatter(c):
+            nc.vector.tensor_tensor(window[:].indirect(dst_sb[:, c * LC : (c + 1) * LC]), y[c][:], gate_sb[:, c * CH : (c + 1) * CH], MULT)
+
+        for j in range(PACK - 1):
+            gather(j, 0, 1)
+            if j == 1:
+                nc.scalar.copy(rounded[:], planes[j][:])
+                nc.scalar.activation(picked[:, j, :], rounded[:].indirect(offs_sb[:, LC:]), COPY)
+            else:
+                gather(j, 1, NCH)
+        last = PACK - 1
+        gather(last, 0, 1)
+        gather(last, 1, 2)
+        product(0)
+        weave(1)
+        activate(0)
+        gather(last, 2, 4)
+        for c in range(1, NCH):
+            product(c)
+            scatter(c - 1)
+            if c + 1 < NCH:
+                weave(c + 1)
+            activate(c)
+        scatter(NCH - 1)
+        nc.sync.dma_start(out, window[:])

@@ -44,34 +44,35 @@ def tile_picked_route2_lingelu_e_kernel(tc, xT, gate, w1_words, w1_scales, offs,
         nc.scalar.activation(bias[:], zero[:], GELU)
 
         x_rows = xT.rearrange("(p j) t -> p j t", j=PACK)
-        nc.sync.dma_start(offs_sb[:], offs)
         for j in range(PACK):
             nc.sync.dma_start(planes[j][:], x_rows[:, j, :])
             if j == 0:
-                nc.sync.dma_start(dst_sb[:], dst)
-        nc.scalar.dma_start(w_codes[:].bitcast(I32), w1_words[0].rearrange("p n t -> p (n t)").bitcast(I32))
+                nc.sync.dma_start(offs_sb[:], offs)
+        nc.sync.dma_start(w_codes[:].bitcast(I32), w1_words[0].rearrange("p n t -> p (n t)").bitcast(I32))
         for q in range(4):
             nc.scalar.dma_start(w_scale[32 * q : 32 * q + 4, :].bitcast(I32), w1_scales[0, 4 * q : 4 * q + 4, :].bitcast(I32))
+        nc.sync.dma_start(dst_sb[:], dst)
         nc.sync.dma_start(gate_sb[:], gate)
 
         rest = S - CH
-        staging = keep.tile([P, PACK * rest - 2 * CH + PACK * CH], BF16, name="staging", align_bytes=64)
+        staging = keep.tile([P, PACK * rest - CH + PACK * CH], BF16, name="staging", align_bytes=64)
         picked = staging[:, : PACK * rest].rearrange("p (j s) -> p j s", j=PACK)
-        woven = [staging[:, PACK * rest - 2 * CH :].rearrange("p (s j) -> p s j", j=PACK)]
-        woven += [keep.tile([P, CH, PACK], BF16, name=f"woven{c}", align_bytes=64)[:] for c in range(1, NCH - 1)]
+        woven = {0: staging[:, PACK * rest - CH :].rearrange("p (s j) -> p s j", j=PACK)}
         rounded = keep.tile([P, T], BF16, name="rounded")
         codes = [keep.tile([P, CH], U32, name=f"codes{c}", tag=f"codes{c}", align_bytes=64) for c in range(NCH)]
         scales = [keep.tile([P, CH], U8, name=f"scales{c}", align_bytes=64) for c in range(NCH)]
-        acc = [psum.tile([P, CH], F32, name=f"acc{c}") for c in range(NCH)]
-        y = [keep.tile([P, CH], F32, name=f"y{c}") for c in range(NCH)]
+        groups = [(0, 1), (1, 2), (2, 4)]
+        banks = [psum.tile([P, (c1 - c0) * CH], F32, name=f"bank{c0}") for c0, c1 in groups]
+        acc = [banks[0][:], banks[1][:], banks[2][:, :CH], banks[2][:, CH:]]
+        y = keep.tile([P, S], F32, name="y")
 
         def gather(j, c0, c1):
             target = woven[0][:, :, j] if c0 == 0 else picked[:, j, (c0 - 1) * CH : (c1 - 1) * CH]
             nc.vector.tensor_copy(target, planes[j][:].indirect(offs_sb[:, c0 * LC : c1 * LC]))
 
         def weave(c):
-            if c == NCH - 1:
-                woven.append(keep.tile([P, CH, PACK], BF16, name=f"woven{c}", tag="codes1", align_bytes=64)[:])
+            tag = "codes0" if c == NCH - 1 else f"woven{c}"
+            woven[c] = keep.tile([P, CH, PACK], BF16, name=f"woven{c}", tag=tag, align_bytes=64)[:]
             nc.scalar.copy(
                 woven[c].rearrange("p (g i) j -> p g j i", i=4),
                 picked[:, :, (c - 1) * CH : c * CH].rearrange("p j (g i) -> p g j i", i=4),
@@ -80,7 +81,7 @@ def tile_picked_route2_lingelu_e_kernel(tc, xT, gate, w1_words, w1_scales, offs,
         def product(c):
             nc.vector.quantize_mx(out=codes[c][:].bitcast(FP8X4), scales=scales[c][:], in_=woven[c].rearrange("p s j -> p (s j)"))
             nc.tensor.matmul_mx(
-                out=acc[c][:],
+                out=acc[c],
                 lhsT=w_codes[:].bitcast(FP8X4),
                 lhsT_scale=w_scale[:],
                 rhs=codes[c][:].bitcast(FP8X4),
@@ -89,11 +90,14 @@ def tile_picked_route2_lingelu_e_kernel(tc, xT, gate, w1_words, w1_scales, offs,
                 stop=True,
             )
 
-        def activate(c):
-            nc.scalar.activation(y[c][:], acc[c][:], GELU, bias=bias[:])
+        def activate(g):
+            c0, c1 = groups[g]
+            nc.scalar.activation(y[:, c0 * CH : c1 * CH], banks[g][:], GELU, bias=bias[:])
 
-        def scatter(c):
-            nc.vector.tensor_tensor(window[:].indirect(dst_sb[:, c * LC : (c + 1) * LC]), y[c][:], gate_sb[:, c * CH : (c + 1) * CH], MULT)
+        def scatter(g):
+            c0, c1 = groups[g]
+            cols = slice(c0 * CH, c1 * CH)
+            nc.vector.tensor_tensor(window[:].indirect(dst_sb[:, c0 * LC : c1 * LC]), y[:, cols], gate_sb[:, cols], MULT)
 
         for j in range(PACK - 1):
             gather(j, 0, 1)
@@ -103,17 +107,21 @@ def tile_picked_route2_lingelu_e_kernel(tc, xT, gate, w1_words, w1_scales, offs,
             else:
                 gather(j, 1, NCH)
         last = PACK - 1
-        gather(last, 0, 1)
         gather(last, 1, 2)
-        product(0)
         weave(1)
+        gather(last, 0, 1)
+        gather(last, 2, 3)
+        weave(2)
+        product(0)
+        product(1)
         activate(0)
-        gather(last, 2, 4)
-        for c in range(1, NCH):
-            product(c)
-            scatter(c - 1)
-            if c + 1 < NCH:
-                weave(c + 1)
-            activate(c)
-        scatter(NCH - 1)
+        gather(last, 3, 4)
+        weave(3)
+        activate(1)
+        product(2)
+        scatter(0)
+        product(3)
+        scatter(1)
+        activate(2)
+        scatter(2)
         nc.sync.dma_start(out, window[:])

@@ -73,7 +73,7 @@ def tile_picked_route2_lingelu_e_kernel(tc, xT, gate, w1_words, w1_scales, offs,
         def weave(c):
             tag = "codes0" if c == NCH - 1 else f"woven{c}"
             woven[c] = keep.tile([P, CH, PACK], BF16, name=f"woven{c}", tag=tag, align_bytes=64)[:]
-            nc.scalar.copy(
+            (nc.vector.tensor_copy if c == 2 else nc.scalar.copy)(
                 woven[c].rearrange("p (g i) j -> p g j i", i=4),
                 picked[:, :, (c - 1) * CH : c * CH].rearrange("p j (g i) -> p g j i", i=4),
             )
@@ -111,12 +111,12 @@ def tile_picked_route2_lingelu_e_kernel(tc, xT, gate, w1_words, w1_scales, offs,
         weave(1)
         gather(last, 0, 1)
         gather(last, 2, 3)
-        weave(2)
         product(0)
-        product(1)
+        weave(2)
         activate(0)
         gather(last, 3, 4)
         weave(3)
+        product(1)
         activate(1)
         product(2)
         scatter(0)

@@ -17,7 +17,6 @@ P = 128
 PACK = 4
 K, T, S, N, U = 512, 1024, 512, 128, 1024
 CH = 128
-NCH = S // CH
 LC = CH // 16
 FLOPS = 2 * K * S * N
 
@@ -30,21 +29,26 @@ def tile_picked_route2_lingelu_e_kernel(tc, xT, gate, w1_words, w1_scales, offs,
 
         offs_sb = keep.tile([P, S // 16], U16, name="offs_sb")
         dst_sb = keep.tile([P, S // 16], U16, name="dst_sb")
-        planes = [keep.tile([P, T], F32, name=f"plane{j}") for j in range(PACK)]
         w_codes = keep.tile([P, N], U32, name="w_codes", align_bytes=64)
         w_scale = keep.tile([P, N], U8, name="w_scale", align_bytes=64)
         gate_sb = keep.tile([P, S], F32, name="gate_sb")
         window = keep.tile([P, U], F32, name="window")
         zero = keep.tile([P, 1], F32, name="zero")
         bias = keep.tile([P, 1], F32, name="bias")
+        planes = [keep.tile([P, T], F32, name=f"plane{j}") for j in range(PACK)]
+        early = keep.tile([P, CH * PACK], BF16, name="early", align_bytes=64)
+        rounded0 = keep.tile([P, T], BF16, name="rounded0")
+        shared = keep.tile([P, T + 3 * CH * PACK], BF16, name="shared", align_bytes=64)
+        SPARE = 16
 
         nc.vector.memset(w_scale[:].bitcast(I32), 0)
         nc.vector.memset(zero[:], 0.0)
+        nc.vector.memset(shared[:, T : T + SPARE], 0.0)
         nc.vector.memset(window[:], 0.0)
         nc.scalar.activation(bias[:], zero[:], GELU)
 
         x_rows = xT.rearrange("(p j) t -> p j t", j=PACK)
-        for j in range(PACK):
+        for j in (0, 2, 1, 3):
             nc.sync.dma_start(planes[j][:], x_rows[:, j, :])
             if j == 0:
                 nc.sync.dma_start(offs_sb[:], offs)
@@ -54,74 +58,60 @@ def tile_picked_route2_lingelu_e_kernel(tc, xT, gate, w1_words, w1_scales, offs,
         nc.sync.dma_start(dst_sb[:], dst)
         nc.sync.dma_start(gate_sb[:], gate)
 
-        rest = S - CH
-        staging = keep.tile([P, PACK * rest - CH + PACK * CH], BF16, name="staging", align_bytes=64)
-        picked = staging[:, : PACK * rest].rearrange("p (j s) -> p j s", j=PACK)
-        woven = {0: staging[:, PACK * rest - CH :].rearrange("p (s j) -> p s j", j=PACK)}
-        rounded = keep.tile([P, T], BF16, name="rounded")
-        codes = [keep.tile([P, CH], U32, name=f"codes{c}", tag=f"codes{c}", align_bytes=64) for c in range(NCH)]
-        scales = [keep.tile([P, CH], U8, name=f"scales{c}", align_bytes=64) for c in range(NCH)]
-        groups = [(0, 1), (1, 2), (2, 4)]
+        groups = [(0, 1), (1, 2), (2, 3), (3, 4)]
+        codes = [keep.tile([P, (c1 - c0) * CH], U32, name=f"codes{c0}", align_bytes=64) for c0, c1 in groups]
+        scales = [keep.tile([P, (c1 - c0) * CH], U8, name=f"scales{c0}", align_bytes=64) for c0, c1 in groups]
         banks = [psum.tile([P, (c1 - c0) * CH], F32, name=f"bank{c0}") for c0, c1 in groups]
-        acc = [banks[0][:], banks[1][:], banks[2][:, :CH], banks[2][:, CH:]]
         y = keep.tile([P, S], F32, name="y")
 
-        def gather(j, c0, c1):
-            target = woven[0][:, :, j] if c0 == 0 else picked[:, j, (c0 - 1) * CH : (c1 - 1) * CH]
-            nc.vector.tensor_copy(target, planes[j][:].indirect(offs_sb[:, c0 * LC : c1 * LC]))
+        def woven(s0, s1):
+            if s0 < CH:
+                return early[:, s0 * PACK : s1 * PACK]
+            return shared[:, T + (s0 - CH) * PACK : T + (s1 - CH) * PACK]
 
-        def weave(c):
-            tag = "codes0" if c == NCH - 1 else f"woven{c}"
-            woven[c] = keep.tile([P, CH, PACK], BF16, name=f"woven{c}", tag=tag, align_bytes=64)[:]
-            (nc.vector.tensor_copy if c == 2 else nc.scalar.copy)(
-                woven[c].rearrange("p (g i) j -> p g j i", i=4),
-                picked[:, :, (c - 1) * CH : c * CH].rearrange("p j (g i) -> p g j i", i=4),
-            )
+        def gather(engine_source, j, s0, s1):
+            target = woven(s0, s1).rearrange("p (s j) -> p s j", j=PACK)[:, :, j]
+            entries = offs_sb[:, s0 // 16 : s1 // 16]
+            if engine_source is None:
+                nc.vector.tensor_copy(target, planes[j][:].indirect(entries))
+            else:
+                nc.scalar.activation(target, engine_source.indirect(entries), COPY)
 
-        def product(c):
-            nc.vector.quantize_mx(out=codes[c][:].bitcast(FP8X4), scales=scales[c][:], in_=woven[c].rearrange("p s j -> p (s j)"))
+        def product(g):
+            c0, c1 = groups[g]
+            nc.vector.quantize_mx(out=codes[g][:].bitcast(FP8X4), scales=scales[g][:], in_=woven(c0 * CH, c1 * CH))
             nc.tensor.matmul_mx(
-                out=acc[c],
+                out=banks[g][:],
                 lhsT=w_codes[:].bitcast(FP8X4),
                 lhsT_scale=w_scale[:],
-                rhs=codes[c][:].bitcast(FP8X4),
-                rhs_scale=scales[c][:],
+                rhs=codes[g][:].bitcast(FP8X4),
+                rhs_scale=scales[g][:],
                 start=True,
                 stop=True,
             )
-
-        def activate(g):
-            c0, c1 = groups[g]
             nc.scalar.activation(y[:, c0 * CH : c1 * CH], banks[g][:], GELU, bias=bias[:])
 
-        def scatter(g):
-            c0, c1 = groups[g]
+        def scatter(c0, c1):
             cols = slice(c0 * CH, c1 * CH)
             nc.vector.tensor_tensor(window[:].indirect(dst_sb[:, c0 * LC : c1 * LC]), y[:, cols], gate_sb[:, cols], MULT)
 
-        for j in range(PACK - 1):
-            gather(j, 0, 1)
-            if j == 1:
-                nc.scalar.copy(rounded[:], planes[j][:])
-                nc.scalar.activation(picked[:, j, :], rounded[:].indirect(offs_sb[:, LC:]), COPY)
-            else:
-                gather(j, 1, NCH)
-        last = PACK - 1
-        gather(last, 1, 2)
-        weave(1)
-        gather(last, 0, 1)
-        gather(last, 2, 3)
+        cut = S - CH - 32
+        nc.vector.tensor_copy(rounded0[:], planes[0][:])
+        gather(None, 0, 0, CH)
+        gather(rounded0[:], 0, CH, S)
+        gather(None, 2, 0, CH)
+        gather(None, 2, CH, S)
+        gather(None, 1, 0, CH)
+        nc.scalar.copy(shared[:, :T], planes[1][:])
+        gather(shared[:, : T + SPARE], 1, cut, S)
+        gather(shared[:, :T], 1, CH, cut)
+        gather(None, 3, 0, CH)
+        gather(None, 3, S - CH, S)
         product(0)
-        weave(2)
-        activate(0)
-        gather(last, 3, 4)
-        weave(3)
-        product(1)
-        activate(1)
-        product(2)
-        scatter(0)
+        gather(None, 3, CH, S - CH)
         product(3)
-        scatter(1)
-        activate(2)
-        scatter(2)
+        product(1)
+        product(2)
+        scatter(0, 1)
+        scatter(1, 4)
         nc.sync.dma_start(out, window[:])

@@ -36,9 +36,8 @@ def tile_picked_route2_lingelu_e_kernel(tc, xT, gate, w1_words, w1_scales, offs,
         zero = keep.tile([P, 1], F32, name="zero")
         bias = keep.tile([P, 1], F32, name="bias")
         planes = [keep.tile([P, T], F32, name=f"plane{j}") for j in range(PACK)]
-        early = keep.tile([P, CH * PACK], BF16, name="early", align_bytes=64)
         rounded0 = keep.tile([P, T], BF16, name="rounded0")
-        shared = keep.tile([P, T + 3 * CH * PACK], BF16, name="shared", align_bytes=64)
+        shared = keep.tile([P, T + S * PACK], BF16, name="shared", align_bytes=64)
         SPARE = 16
 
         nc.vector.memset(w_scale[:].bitcast(I32), 0)
@@ -65,9 +64,7 @@ def tile_picked_route2_lingelu_e_kernel(tc, xT, gate, w1_words, w1_scales, offs,
         y = keep.tile([P, S], F32, name="y")
 
         def woven(s0, s1):
-            if s0 < CH:
-                return early[:, s0 * PACK : s1 * PACK]
-            return shared[:, T + (s0 - CH) * PACK : T + (s1 - CH) * PACK]
+            return shared[:, T + s0 * PACK : T + s1 * PACK]
 
         def gather(engine_source, j, s0, s1):
             target = woven(s0, s1).rearrange("p (s j) -> p s j", j=PACK)[:, :, j]
@@ -95,23 +92,26 @@ def tile_picked_route2_lingelu_e_kernel(tc, xT, gate, w1_words, w1_scales, offs,
             cols = slice(c0 * CH, c1 * CH)
             nc.vector.tensor_tensor(window[:].indirect(dst_sb[:, c0 * LC : c1 * LC]), y[:, cols], gate_sb[:, cols], MULT)
 
-        cut = S - CH - 32
+        own = 320
+        held = 192
+        cut = 160
         nc.vector.tensor_copy(rounded0[:], planes[0][:])
-        gather(None, 0, 0, CH)
-        gather(rounded0[:], 0, CH, S)
-        gather(None, 2, 0, CH)
-        gather(None, 2, CH, S)
-        gather(None, 1, 0, CH)
-        nc.scalar.copy(shared[:, :T], planes[1][:])
-        gather(shared[:, : T + SPARE], 1, cut, S)
-        gather(shared[:, :T], 1, CH, cut)
-        gather(None, 3, 0, CH)
-        gather(None, 3, S - CH, S)
-        product(0)
-        gather(None, 3, CH, S - CH)
+        gather(None, 0, own, S)
+        gather(rounded0[:], 0, 0, own)
+        gather(None, 2, 0, S)
+        split = 7 * T // 8
+        nc.vector.tensor_copy(shared[:, split:T], planes[1][:, split:])
+        gather(None, 1, own, S)
+        nc.scalar.copy(shared[:, :split], planes[1][:, :split])
+        gather(shared[:, : T + SPARE], 1, cut, own)
+        gather(shared[:, :T], 1, 0, cut)
+        gather(None, 3, 3 * CH, S)
+        gather(None, 3, held, 3 * CH)
         product(3)
-        product(1)
+        gather(None, 3, 0, held)
         product(2)
-        scatter(0, 1)
-        scatter(1, 4)
+        product(1)
+        product(0)
+        scatter(3, 4)
+        scatter(0, 3)
         nc.sync.dma_start(out, window[:])

@@ -92,9 +92,9 @@ def tile_picked_route2_lingelu_e_kernel(tc, xT, gate, w1_words, w1_scales, offs,
             cols = slice(c0 * CH, c1 * CH)
             nc.vector.tensor_tensor(window[:].indirect(dst_sb[:, c0 * LC : c1 * LC]), y[:, cols], gate_sb[:, cols], MULT)
 
-        own = 320
+        own = 352
         held = 192
-        cut = 160
+        cut = 192
         nc.vector.tensor_copy(rounded0[:], planes[0][:])
         gather(None, 0, own, S)
         gather(rounded0[:], 0, 0, own)

@@ -16,9 +16,15 @@ MULT = mybir.AluOpType.mult
 P = 128
 PACK = 4
 K, T, S, N, U = 512, 1024, 512, 128, 1024
-CH = 128
-LC = CH // 16
+STRIPE = 16
+GROUP = 128
 FLOPS = 2 * K * S * N
+
+SCALAR_END = 352
+SCALAR_CUT = 192
+ROUND_CUT = 7 * T // 8
+HELD = 192
+SPARE = 16
 
 
 def tile_picked_route2_lingelu_e_kernel(tc, xT, gate, w1_words, w1_scales, offs, dst, out):
@@ -27,91 +33,88 @@ def tile_picked_route2_lingelu_e_kernel(tc, xT, gate, w1_words, w1_scales, offs,
         keep = ctx.enter_context(tc.tile_pool(name="keep", bufs=1))
         psum = ctx.enter_context(tc.psum_pool(name="psum", bufs=1))
 
-        offs_sb = keep.tile([P, S // 16], U16, name="offs_sb")
-        dst_sb = keep.tile([P, S // 16], U16, name="dst_sb")
+        offs_sb = keep.tile([P, S // STRIPE], U16, name="offs_sb")
+        dst_sb = keep.tile([P, S // STRIPE], U16, name="dst_sb")
         w_codes = keep.tile([P, N], U32, name="w_codes", align_bytes=64)
         w_scale = keep.tile([P, N], U8, name="w_scale", align_bytes=64)
         gate_sb = keep.tile([P, S], F32, name="gate_sb")
-        window = keep.tile([P, U], F32, name="window")
+        placed = keep.tile([P, U], F32, name="placed")
         zero = keep.tile([P, 1], F32, name="zero")
         bias = keep.tile([P, 1], F32, name="bias")
         planes = [keep.tile([P, T], F32, name=f"plane{j}") for j in range(PACK)]
         rounded0 = keep.tile([P, T], BF16, name="rounded0")
-        shared = keep.tile([P, T + S * PACK], BF16, name="shared", align_bytes=64)
-        SPARE = 16
+        rounded1_picked = keep.tile([P, T + S * PACK], BF16, name="rounded1_picked", align_bytes=64)
+        y = keep.tile([P, S], F32, name="y")
 
         nc.vector.memset(w_scale[:].bitcast(I32), 0)
         nc.vector.memset(zero[:], 0.0)
-        nc.vector.memset(shared[:, T : T + SPARE], 0.0)
-        nc.vector.memset(window[:], 0.0)
+        nc.vector.memset(placed[:], 0.0)
         nc.scalar.activation(bias[:], zero[:], GELU)
 
         x_rows = xT.rearrange("(p j) t -> p j t", j=PACK)
-        for j in (0, 2, 1, 3):
+        nc.sync.dma_start(planes[0][:], x_rows[:, 0, :])
+        nc.sync.dma_start(offs_sb[:], offs)
+        for j in (2, 1, 3):
             nc.sync.dma_start(planes[j][:], x_rows[:, j, :])
-            if j == 0:
-                nc.sync.dma_start(offs_sb[:], offs)
         nc.sync.dma_start(w_codes[:].bitcast(I32), w1_words[0].rearrange("p n t -> p (n t)").bitcast(I32))
         for q in range(4):
             nc.scalar.dma_start(w_scale[32 * q : 32 * q + 4, :].bitcast(I32), w1_scales[0, 4 * q : 4 * q + 4, :].bitcast(I32))
         nc.sync.dma_start(dst_sb[:], dst)
         nc.sync.dma_start(gate_sb[:], gate)
 
-        groups = [(0, 1), (1, 2), (2, 3), (3, 4)]
-        codes = [keep.tile([P, (c1 - c0) * CH], U32, name=f"codes{c0}", align_bytes=64) for c0, c1 in groups]
-        scales = [keep.tile([P, (c1 - c0) * CH], U8, name=f"scales{c0}", align_bytes=64) for c0, c1 in groups]
-        banks = [psum.tile([P, (c1 - c0) * CH], F32, name=f"bank{c0}") for c0, c1 in groups]
-        y = keep.tile([P, S], F32, name="y")
+        def picked(s0, s1):
+            return rounded1_picked[:, T + s0 * PACK : T + s1 * PACK]
 
-        def woven(s0, s1):
-            return shared[:, T + s0 * PACK : T + s1 * PACK]
+        def slot(j, s0, s1):
+            return picked(s0, s1).rearrange("p (s j) -> p s j", j=PACK)[:, :, j]
 
-        def gather(engine_source, j, s0, s1):
-            target = woven(s0, s1).rearrange("p (s j) -> p s j", j=PACK)[:, :, j]
-            entries = offs_sb[:, s0 // 16 : s1 // 16]
-            if engine_source is None:
-                nc.vector.tensor_copy(target, planes[j][:].indirect(entries))
-            else:
-                nc.scalar.activation(target, engine_source.indirect(entries), COPY)
+        def gather_on_vector(j, s0, s1):
+            nc.vector.tensor_copy(slot(j, s0, s1), planes[j][:].indirect(offs_sb[:, s0 // STRIPE : s1 // STRIPE]))
+
+        def gather_on_scalar(rounded, j, s0, s1):
+            nc.scalar.activation(slot(j, s0, s1), rounded.indirect(offs_sb[:, s0 // STRIPE : s1 // STRIPE]), COPY)
 
         def product(g):
-            c0, c1 = groups[g]
-            nc.vector.quantize_mx(out=codes[g][:].bitcast(FP8X4), scales=scales[g][:], in_=woven(c0 * CH, c1 * CH))
+            s0, s1 = g * GROUP, (g + 1) * GROUP
+            codes = keep.tile([P, GROUP], U32, name=f"codes{g}", align_bytes=64)
+            scales = keep.tile([P, GROUP], U8, name=f"scales{g}", align_bytes=64)
+            bank = psum.tile([P, GROUP], F32, name=f"bank{g}")
+            nc.vector.quantize_mx(out=codes[:].bitcast(FP8X4), scales=scales[:], in_=picked(s0, s1))
             nc.tensor.matmul_mx(
-                out=banks[g][:],
+                out=bank[:],
                 lhsT=w_codes[:].bitcast(FP8X4),
                 lhsT_scale=w_scale[:],
-                rhs=codes[g][:].bitcast(FP8X4),
-                rhs_scale=scales[g][:],
+                rhs=codes[:].bitcast(FP8X4),
+                rhs_scale=scales[:],
                 start=True,
                 stop=True,
             )
-            nc.scalar.activation(y[:, c0 * CH : c1 * CH], banks[g][:], GELU, bias=bias[:])
+            nc.scalar.activation(y[:, s0:s1], bank[:], GELU, bias=bias[:])
 
-        def scatter(c0, c1):
-            cols = slice(c0 * CH, c1 * CH)
-            nc.vector.tensor_tensor(window[:].indirect(dst_sb[:, c0 * LC : c1 * LC]), y[:, cols], gate_sb[:, cols], MULT)
+        def scatter(s0, s1):
+            places = placed[:].indirect(dst_sb[:, s0 // STRIPE : s1 // STRIPE])
+            nc.vector.tensor_tensor(places, y[:, s0:s1], gate_sb[:, s0:s1], MULT)
 
-        own = 352
-        held = 192
-        cut = 192
         nc.vector.tensor_copy(rounded0[:], planes[0][:])
-        gather(None, 0, own, S)
-        gather(rounded0[:], 0, 0, own)
-        gather(None, 2, 0, S)
-        split = 7 * T // 8
-        nc.vector.tensor_copy(shared[:, split:T], planes[1][:, split:])
-        gather(None, 1, own, S)
-        nc.scalar.copy(shared[:, :split], planes[1][:, :split])
-        gather(shared[:, : T + SPARE], 1, cut, own)
-        gather(shared[:, :T], 1, 0, cut)
-        gather(None, 3, 3 * CH, S)
-        gather(None, 3, held, 3 * CH)
-        product(3)
-        gather(None, 3, 0, held)
-        product(2)
-        product(1)
-        product(0)
-        scatter(3, 4)
-        scatter(0, 3)
-        nc.sync.dma_start(out, window[:])
+        gather_on_vector(0, SCALAR_END, S)
+        gather_on_scalar(rounded0[:], 0, 0, SCALAR_END)
+
+        gather_on_vector(2, 0, S)
+
+        nc.vector.tensor_copy(rounded1_picked[:, ROUND_CUT:T], planes[1][:, ROUND_CUT:])
+        gather_on_vector(1, SCALAR_END, S)
+        nc.scalar.copy(rounded1_picked[:, :ROUND_CUT], planes[1][:, :ROUND_CUT])
+        gather_on_scalar(rounded1_picked[:, : T + SPARE], 1, SCALAR_CUT, SCALAR_END)
+        gather_on_scalar(rounded1_picked[:, :T], 1, 0, SCALAR_CUT)
+
+        last = S // GROUP - 1
+        gather_on_vector(3, last * GROUP, S)
+        gather_on_vector(3, HELD, last * GROUP)
+        product(last)
+        gather_on_vector(3, 0, HELD)
+        for g in reversed(range(last)):
+            product(g)
+
+        scatter(last * GROUP, S)
+        scatter(0, last * GROUP)
+        nc.sync.dma_start(out, placed[:])

@@ -20,11 +20,10 @@ STRIPE = 16
 GROUP = 128
 FLOPS = 2 * K * S * N
 
-SCALAR_END = 352
-SCALAR_CUT = 192
-ROUND_CUT = 7 * T // 8
-HELD = 192
-SPARE = 16
+REST = S - GROUP
+SCALAR_END = 192
+HELD = 2 * GROUP
+ROUND_CUT = 3 * T // 4
 
 
 def tile_picked_route2_lingelu_e_kernel(tc, xT, gate, w1_words, w1_scales, offs, dst, out):
@@ -37,13 +36,15 @@ def tile_picked_route2_lingelu_e_kernel(tc, xT, gate, w1_words, w1_scales, offs,
         dst_sb = keep.tile([P, S // STRIPE], U16, name="dst_sb")
         w_codes = keep.tile([P, N], U32, name="w_codes", align_bytes=64)
         w_scale = keep.tile([P, N], U8, name="w_scale", align_bytes=64)
-        gate_sb = keep.tile([P, S], F32, name="gate_sb")
+        last_gate = keep.tile([P, T + S], F32, name="last_gate")
+        gate_sb = last_gate[:, T:]
         placed = keep.tile([P, U], F32, name="placed")
         zero = keep.tile([P, 1], F32, name="zero")
         bias = keep.tile([P, 1], F32, name="bias")
-        planes = [keep.tile([P, T], F32, name=f"plane{j}") for j in range(PACK)]
-        rounded0 = keep.tile([P, T], BF16, name="rounded0")
-        rounded1_picked = keep.tile([P, T + S * PACK], BF16, name="rounded1_picked", align_bytes=64)
+        planes = [keep.tile([P, T], F32, name=f"plane{j}")[:] for j in range(PACK - 1)] + [last_gate[:, :T]]
+        rounded = [keep.tile([P, T], BF16, name=f"rounded{j}") for j in range(2)]
+        pairs = keep.tile([P, 2, 2 * GROUP], BF16, name="pairs")
+        values = keep.tile([P, S * PACK], BF16, name="values", align_bytes=64)
         y = keep.tile([P, S], F32, name="y")
 
         nc.vector.memset(w_scale[:].bitcast(I32), 0)
@@ -52,34 +53,38 @@ def tile_picked_route2_lingelu_e_kernel(tc, xT, gate, w1_words, w1_scales, offs,
         nc.scalar.activation(bias[:], zero[:], GELU)
 
         x_rows = xT.rearrange("(p j) t -> p j t", j=PACK)
-        nc.sync.dma_start(planes[0][:], x_rows[:, 0, :])
+        nc.sync.dma_start(planes[0], x_rows[:, 0, :])
         nc.sync.dma_start(offs_sb[:], offs)
         for j in (2, 1, 3):
-            nc.sync.dma_start(planes[j][:], x_rows[:, j, :])
+            nc.sync.dma_start(planes[j], x_rows[:, j, :])
+        nc.sync.dma_start(gate_sb, gate)
         nc.sync.dma_start(w_codes[:].bitcast(I32), w1_words[0].rearrange("p n t -> p (n t)").bitcast(I32))
         for q in range(4):
             nc.scalar.dma_start(w_scale[32 * q : 32 * q + 4, :].bitcast(I32), w1_scales[0, 4 * q : 4 * q + 4, :].bitcast(I32))
         nc.sync.dma_start(dst_sb[:], dst)
-        nc.sync.dma_start(gate_sb[:], gate)
 
-        def picked(s0, s1):
-            return rounded1_picked[:, T + s0 * PACK : T + s1 * PACK]
+        def entries(s0, s1):
+            return offs_sb[:, s0 // STRIPE : s1 // STRIPE]
 
         def slot(j, s0, s1):
-            return picked(s0, s1).rearrange("p (s j) -> p s j", j=PACK)[:, :, j]
+            return values[:, s0 * PACK : s1 * PACK].rearrange("p (s j) -> p s j", j=PACK)[:, :, j]
 
-        def gather_on_vector(j, s0, s1):
-            nc.vector.tensor_copy(slot(j, s0, s1), planes[j][:].indirect(offs_sb[:, s0 // STRIPE : s1 // STRIPE]))
+        def gather(j, s0, s1, window):
+            nc.vector.tensor_copy(slot(j, s0, s1), window.indirect(entries(s0, s1)))
 
-        def gather_on_scalar(rounded, j, s0, s1):
-            nc.scalar.activation(slot(j, s0, s1), rounded.indirect(offs_sb[:, s0 // STRIPE : s1 // STRIPE]), COPY)
+        def gather_pair(j):
+            half = pairs[:, j // 2, :].rearrange("p (s e) -> p s e", e=2)[:, :, j % 2]
+            nc.vector.tensor_copy(half, planes[j].indirect(entries(0, GROUP)))
+
+        def gather_on_scalar(j):
+            nc.scalar.activation(slot(j, GROUP, REST), rounded[j][:].indirect(entries(GROUP, REST)), COPY)
 
         def product(g):
             s0, s1 = g * GROUP, (g + 1) * GROUP
             codes = keep.tile([P, GROUP], U32, name=f"codes{g}", align_bytes=64)
             scales = keep.tile([P, GROUP], U8, name=f"scales{g}", align_bytes=64)
             bank = psum.tile([P, GROUP], F32, name=f"bank{g}")
-            nc.vector.quantize_mx(out=codes[:].bitcast(FP8X4), scales=scales[:], in_=picked(s0, s1))
+            nc.vector.quantize_mx(out=codes[:].bitcast(FP8X4), scales=scales[:], in_=values[:, s0 * PACK : s1 * PACK])
             nc.tensor.matmul_mx(
                 out=bank[:],
                 lhsT=w_codes[:].bitcast(FP8X4),
@@ -95,26 +100,26 @@ def tile_picked_route2_lingelu_e_kernel(tc, xT, gate, w1_words, w1_scales, offs,
             places = placed[:].indirect(dst_sb[:, s0 // STRIPE : s1 // STRIPE])
             nc.vector.tensor_tensor(places, y[:, s0:s1], gate_sb[:, s0:s1], MULT)
 
-        nc.vector.tensor_copy(rounded0[:], planes[0][:])
-        gather_on_vector(0, SCALAR_END, S)
-        gather_on_scalar(rounded0[:], 0, 0, SCALAR_END)
+        nc.scalar.copy(rounded[0][:], planes[0])
+        gather_on_scalar(0)
+        gather(0, REST, S, planes[0])
+        gather_pair(0)
+        gather(2, GROUP, S, planes[2])
+        gather_pair(2)
+        nc.vector.tensor_copy(rounded[1][:, ROUND_CUT:], planes[1][:, ROUND_CUT:])
+        gather(1, REST, S, planes[1])
+        gather_pair(1)
+        nc.scalar.copy(rounded[1][:, :ROUND_CUT], planes[1][:, :ROUND_CUT])
+        gather_on_scalar(1)
 
-        gather_on_vector(2, 0, S)
-
-        nc.vector.tensor_copy(rounded1_picked[:, ROUND_CUT:T], planes[1][:, ROUND_CUT:])
-        gather_on_vector(1, SCALAR_END, S)
-        nc.scalar.copy(rounded1_picked[:, :ROUND_CUT], planes[1][:, :ROUND_CUT])
-        gather_on_scalar(rounded1_picked[:, : T + SPARE], 1, SCALAR_CUT, SCALAR_END)
-        gather_on_scalar(rounded1_picked[:, :T], 1, 0, SCALAR_CUT)
-
-        last = S // GROUP - 1
-        gather_on_vector(3, last * GROUP, S)
-        gather_on_vector(3, HELD, last * GROUP)
-        product(last)
-        gather_on_vector(3, 0, HELD)
-        for g in reversed(range(last)):
+        gather(3, REST, S, planes[3])
+        gather_pair(3)
+        woven = values[:, : GROUP * PACK].bitcast(U32).rearrange("p (s u) -> p s u", u=2)
+        nc.scalar.copy(woven, pairs[:].bitcast(U32).rearrange("p u s -> p s u"))
+        product(3)
+        gather(3, GROUP, REST, last_gate[:, : T + 8])
+        for g in (0, 2, 1):
             product(g)
-
-        scatter(last * GROUP, S)
-        scatter(0, last * GROUP)
+        scatter(REST, S)
+        scatter(0, REST)
         nc.sync.dma_start(out, placed[:])

@@ -22,8 +22,8 @@ FLOPS = 2 * K * S * N
 
 REST = S - GROUP
 SCALAR_END = 192
-HELD = 2 * GROUP
-ROUND_CUT = 3 * T // 4
+PAIRED = 224
+ROUND_CUT = T
 
 
 def tile_picked_route2_lingelu_e_kernel(tc, xT, gate, w1_words, w1_scales, offs, dst, out):
@@ -43,7 +43,7 @@ def tile_picked_route2_lingelu_e_kernel(tc, xT, gate, w1_words, w1_scales, offs,
         bias = keep.tile([P, 1], F32, name="bias")
         planes = [keep.tile([P, T], F32, name=f"plane{j}")[:] for j in range(PACK - 1)] + [last_gate[:, :T]]
         rounded = [keep.tile([P, T], BF16, name=f"rounded{j}") for j in range(2)]
-        pairs = keep.tile([P, 2, 2 * GROUP], BF16, name="pairs")
+        pairs = keep.tile([P, 2, 2 * PAIRED], BF16, name="pairs")
         values = keep.tile([P, S * PACK], BF16, name="values", align_bytes=64)
         y = keep.tile([P, S], F32, name="y")
 
@@ -74,10 +74,10 @@ def tile_picked_route2_lingelu_e_kernel(tc, xT, gate, w1_words, w1_scales, offs,
 
         def gather_pair(j):
             half = pairs[:, j // 2, :].rearrange("p (s e) -> p s e", e=2)[:, :, j % 2]
-            nc.vector.tensor_copy(half, planes[j].indirect(entries(0, GROUP)))
+            nc.vector.tensor_copy(half, planes[j].indirect(entries(0, PAIRED)))
 
         def gather_on_scalar(j):
-            nc.scalar.activation(slot(j, GROUP, REST), rounded[j][:].indirect(entries(GROUP, REST)), COPY)
+            nc.scalar.activation(slot(j, PAIRED, REST), rounded[j][:].indirect(entries(PAIRED, REST)), COPY)
 
         def product(g):
             s0, s1 = g * GROUP, (g + 1) * GROUP
@@ -104,9 +104,8 @@ def tile_picked_route2_lingelu_e_kernel(tc, xT, gate, w1_words, w1_scales, offs,
         gather_on_scalar(0)
         gather(0, REST, S, planes[0])
         gather_pair(0)
-        gather(2, GROUP, S, planes[2])
+        gather(2, PAIRED, S, planes[2])
         gather_pair(2)
-        nc.vector.tensor_copy(rounded[1][:, ROUND_CUT:], planes[1][:, ROUND_CUT:])
         gather(1, REST, S, planes[1])
         gather_pair(1)
         nc.scalar.copy(rounded[1][:, :ROUND_CUT], planes[1][:, :ROUND_CUT])
@@ -114,10 +113,11 @@ def tile_picked_route2_lingelu_e_kernel(tc, xT, gate, w1_words, w1_scales, offs,
 
         gather(3, REST, S, planes[3])
         gather_pair(3)
-        woven = values[:, : GROUP * PACK].bitcast(U32).rearrange("p (s u) -> p s u", u=2)
-        nc.scalar.copy(woven, pairs[:].bitcast(U32).rearrange("p u s -> p s u"))
+        for s0, s1 in ((0, GROUP), (GROUP, PAIRED)):
+            woven = values[:, s0 * PACK : s1 * PACK].bitcast(U32).rearrange("p (c i u) -> p c u i", i=4, u=2)
+            nc.scalar.copy(woven, pairs[:].bitcast(U32)[:, :, s0:s1].rearrange("p u (c i) -> p c u i", i=4))
         product(3)
-        gather(3, GROUP, REST, last_gate[:, : T + 8])
+        gather(3, PAIRED, REST, last_gate[:, : T + 8])
         for g in (0, 2, 1):
             product(g)
         scatter(REST, S)

@@ -18,12 +18,13 @@ PACK = 4
 K, T, S, N, U = 512, 1024, 512, 128, 1024
 STRIPE = 16
 GROUP = 128
+LEAD = S - GROUP
 FLOPS = 2 * K * S * N
 
-REST = S - GROUP
-SCALAR_END = 192
 PAIRED = 224
-ROUND_CUT = T
+SCALAR_ROUNDS = (T // 2, 3 * T // 4)
+SPARE = 8
+LINE = 4
 
 
 def tile_picked_route2_lingelu_e_kernel(tc, xT, gate, w1_words, w1_scales, offs, dst, out):
@@ -36,12 +37,12 @@ def tile_picked_route2_lingelu_e_kernel(tc, xT, gate, w1_words, w1_scales, offs,
         dst_sb = keep.tile([P, S // STRIPE], U16, name="dst_sb")
         w_codes = keep.tile([P, N], U32, name="w_codes", align_bytes=64)
         w_scale = keep.tile([P, N], U8, name="w_scale", align_bytes=64)
-        last_gate = keep.tile([P, T + S], F32, name="last_gate")
-        gate_sb = last_gate[:, T:]
+        plane3_gate = keep.tile([P, T + S], F32, name="plane3_gate")
+        gate_sb = plane3_gate[:, T:]
         placed = keep.tile([P, U], F32, name="placed")
         zero = keep.tile([P, 1], F32, name="zero")
         bias = keep.tile([P, 1], F32, name="bias")
-        planes = [keep.tile([P, T], F32, name=f"plane{j}")[:] for j in range(PACK - 1)] + [last_gate[:, :T]]
+        planes = [keep.tile([P, T], F32, name=f"plane{j}")[:] for j in range(PACK - 1)] + [plane3_gate[:, :T]]
         rounded = [keep.tile([P, T], BF16, name=f"rounded{j}") for j in range(2)]
         pairs = keep.tile([P, 2, 2 * PAIRED], BF16, name="pairs")
         values = keep.tile([P, S * PACK], BF16, name="values", align_bytes=64)
@@ -69,15 +70,24 @@ def tile_picked_route2_lingelu_e_kernel(tc, xT, gate, w1_words, w1_scales, offs,
         def slot(j, s0, s1):
             return values[:, s0 * PACK : s1 * PACK].rearrange("p (s j) -> p s j", j=PACK)[:, :, j]
 
-        def gather(j, s0, s1, window):
+        def round_plane(j):
+            cut = SCALAR_ROUNDS[j]
+            nc.vector.tensor_copy(rounded[j][:, cut:], planes[j][:, cut:])
+            nc.scalar.copy(rounded[j][:, :cut], planes[j][:, :cut])
+
+        def gather_on_vector(j, s0, s1, window):
             nc.vector.tensor_copy(slot(j, s0, s1), window.indirect(entries(s0, s1)))
 
-        def gather_pair(j):
-            half = pairs[:, j // 2, :].rearrange("p (s e) -> p s e", e=2)[:, :, j % 2]
-            nc.vector.tensor_copy(half, planes[j].indirect(entries(0, PAIRED)))
+        def gather_on_scalar(j, s0, s1):
+            nc.scalar.activation(slot(j, s0, s1), rounded[j][:].indirect(entries(s0, s1)), COPY)
 
-        def gather_on_scalar(j):
-            nc.scalar.activation(slot(j, PAIRED, REST), rounded[j][:].indirect(entries(PAIRED, REST)), COPY)
+        def gather_pairs(j):
+            every_second = pairs[:, j // 2, :].rearrange("p (s e) -> p s e", e=2)[:, :, j % 2]
+            nc.vector.tensor_copy(every_second, planes[j].indirect(entries(0, PAIRED)))
+
+        def interleave(s0, s1):
+            words = values[:, s0 * PACK : s1 * PACK].bitcast(U32).rearrange("p (c i u) -> p c u i", i=LINE, u=2)
+            nc.scalar.copy(words, pairs[:].bitcast(U32)[:, :, s0:s1].rearrange("p u (c i) -> p c u i", i=LINE))
 
         def product(g):
             s0, s1 = g * GROUP, (g + 1) * GROUP
@@ -100,26 +110,27 @@ def tile_picked_route2_lingelu_e_kernel(tc, xT, gate, w1_words, w1_scales, offs,
             places = placed[:].indirect(dst_sb[:, s0 // STRIPE : s1 // STRIPE])
             nc.vector.tensor_tensor(places, y[:, s0:s1], gate_sb[:, s0:s1], MULT)
 
-        nc.scalar.copy(rounded[0][:], planes[0])
-        gather_on_scalar(0)
-        gather(0, REST, S, planes[0])
-        gather_pair(0)
-        gather(2, PAIRED, S, planes[2])
-        gather_pair(2)
-        gather(1, REST, S, planes[1])
-        gather_pair(1)
-        nc.scalar.copy(rounded[1][:, :ROUND_CUT], planes[1][:, :ROUND_CUT])
-        gather_on_scalar(1)
+        round_plane(0)
+        gather_on_scalar(0, PAIRED, S)
+        gather_pairs(0)
 
-        gather(3, REST, S, planes[3])
-        gather_pair(3)
-        for s0, s1 in ((0, GROUP), (GROUP, PAIRED)):
-            woven = values[:, s0 * PACK : s1 * PACK].bitcast(U32).rearrange("p (c i u) -> p c u i", i=4, u=2)
-            nc.scalar.copy(woven, pairs[:].bitcast(U32)[:, :, s0:s1].rearrange("p u (c i) -> p c u i", i=4))
-        product(3)
-        gather(3, PAIRED, REST, last_gate[:, : T + 8])
+        gather_on_vector(2, PAIRED, S, planes[2])
+        gather_pairs(2)
+
+        round_plane(1)
+        gather_on_scalar(1, LEAD, S)
+        gather_on_scalar(1, PAIRED, LEAD)
+        gather_pairs(1)
+
+        gather_on_vector(3, LEAD, S, planes[3])
+        gather_pairs(3)
+        interleave(0, GROUP)
+        interleave(GROUP, PAIRED)
+        product(LEAD // GROUP)
+        gather_on_vector(3, PAIRED, LEAD, plane3_gate[:, : T + SPARE])
         for g in (0, 2, 1):
             product(g)
-        scatter(REST, S)
-        scatter(0, REST)
+
+        scatter(LEAD, S)
+        scatter(0, LEAD)
         nc.sync.dma_start(out, placed[:])

@@ -22,7 +22,7 @@ LEAD = S - GROUP
 FLOPS = 2 * K * S * N
 
 PAIRED = 224
-SCALAR_ROUNDS = (T // 2, 3 * T // 4)
+SCALAR_ROUNDS = (T // 2, 5 * T // 8)
 SPARE = 8
 LINE = 4
 
@@ -72,7 +72,7 @@ def tile_picked_route2_lingelu_e_kernel(tc, xT, gate, w1_words, w1_scales, offs,
 
         def round_plane(j):
             cut = SCALAR_ROUNDS[j]
-            nc.vector.tensor_copy(rounded[j][:, cut:], planes[j][:, cut:])
+            nc.gpsimd.tensor_copy(rounded[j][:, cut:], planes[j][:, cut:])
             nc.scalar.copy(rounded[j][:, :cut], planes[j][:, :cut])
 
         def gather_on_vector(j, s0, s1, window):
@@ -89,12 +89,14 @@ def tile_picked_route2_lingelu_e_kernel(tc, xT, gate, w1_words, w1_scales, offs,
             words = values[:, s0 * PACK : s1 * PACK].bitcast(U32).rearrange("p (c i u) -> p c u i", i=LINE, u=2)
             nc.scalar.copy(words, pairs[:].bitcast(U32)[:, :, s0:s1].rearrange("p u (c i) -> p c u i", i=LINE))
 
-        def product(g):
-            s0, s1 = g * GROUP, (g + 1) * GROUP
-            codes = keep.tile([P, GROUP], U32, name=f"codes{g}", align_bytes=64)
-            scales = keep.tile([P, GROUP], U8, name=f"scales{g}", align_bytes=64)
-            bank = psum.tile([P, GROUP], F32, name=f"bank{g}")
-            nc.vector.quantize_mx(out=codes[:].bitcast(FP8X4), scales=scales[:], in_=values[:, s0 * PACK : s1 * PACK])
+        def product(s0, s1, parts=1):
+            codes = keep.tile([P, s1 - s0], U32, name=f"codes{s0}", align_bytes=64)
+            scales = keep.tile([P, s1 - s0], U8, name=f"scales{s0}", align_bytes=64)
+            bank = psum.tile([P, s1 - s0], F32, name=f"bank{s0}")
+            width = (s1 - s0) // parts
+            for c in range(0, s1 - s0, width):
+                part = values[:, (s0 + c) * PACK : (s0 + c + width) * PACK]
+                nc.vector.quantize_mx(out=codes[:, c : c + width].bitcast(FP8X4), scales=scales[:, c : c + width], in_=part)
             nc.tensor.matmul_mx(
                 out=bank[:],
                 lhsT=w_codes[:].bitcast(FP8X4),
@@ -124,12 +126,14 @@ def tile_picked_route2_lingelu_e_kernel(tc, xT, gate, w1_words, w1_scales, offs,
 
         gather_on_vector(3, LEAD, S, planes[3])
         gather_pairs(3)
-        interleave(0, GROUP)
+        interleave(0, GROUP // 2)
+        interleave(GROUP // 2, GROUP)
         interleave(GROUP, PAIRED)
-        product(LEAD // GROUP)
+        product(LEAD, LEAD + GROUP // 2)
+        product(LEAD + GROUP // 2, S)
         gather_on_vector(3, PAIRED, LEAD, plane3_gate[:, : T + SPARE])
         for g in (0, 2, 1):
-            product(g)
+            product(g * GROUP, (g + 1) * GROUP, 2 if g == 0 else 1)
 
         scatter(LEAD, S)
         scatter(0, LEAD)

@@ -12,19 +12,17 @@ FP8X4 = mybir.dt.float8_e4m3fn_x4
 GELU = mybir.ActivationFunctionType.Gelu_apprx_tanh
 COPY = mybir.ActivationFunctionType.Copy
 MULT = mybir.AluOpType.mult
+ADD = mybir.AluOpType.add
 
 P = 128
 PACK = 4
 K, T, S, N, U = 512, 1024, 512, 128, 1024
 STRIPE = 16
 GROUP = 128
-LEAD = S - GROUP
+LEAD = GROUP
+SCALAR_PLACES = S // 2
+PIECES = (256, 256, 256, 256)
 FLOPS = 2 * K * S * N
-
-PAIRED = 224
-SCALAR_ROUNDS = (T // 2, 5 * T // 8)
-SPARE = 8
-LINE = 4
 
 
 def tile_picked_route2_lingelu_e_kernel(tc, xT, gate, w1_words, w1_scales, offs, dst, out):
@@ -37,66 +35,60 @@ def tile_picked_route2_lingelu_e_kernel(tc, xT, gate, w1_words, w1_scales, offs,
         dst_sb = keep.tile([P, S // STRIPE], U16, name="dst_sb")
         w_codes = keep.tile([P, N], U32, name="w_codes", align_bytes=64)
         w_scale = keep.tile([P, N], U8, name="w_scale", align_bytes=64)
-        plane3_gate = keep.tile([P, T + S], F32, name="plane3_gate")
-        gate_sb = plane3_gate[:, T:]
-        placed = keep.tile([P, U], F32, name="placed")
+        gate_sb = keep.tile([P, S], F32, name="gate_sb")
         zero = keep.tile([P, 1], F32, name="zero")
         bias = keep.tile([P, 1], F32, name="bias")
-        planes = [keep.tile([P, T], F32, name=f"plane{j}")[:] for j in range(PACK - 1)] + [plane3_gate[:, :T]]
-        rounded = [keep.tile([P, T], BF16, name=f"rounded{j}") for j in range(2)]
-        pairs = keep.tile([P, 2, 2 * PAIRED], BF16, name="pairs")
-        values = keep.tile([P, S * PACK], BF16, name="values", align_bytes=64)
+        planes = [keep.tile([P, T], F32, name=f"plane{j}") for j in range(PACK)]
+        rows01 = keep.tile([P, 2, S - LEAD], BF16, name="rows01")
+        rows23 = {s0: keep.tile([P, 2, GROUP], BF16, name=f"rows23_{s0}") for s0 in range(LEAD, S, GROUP)}
+        values = {s0: keep.tile([P, GROUP * PACK], BF16, name=f"values{s0}", align_bytes=64) for s0 in range(0, S, GROUP)}
         y = keep.tile([P, S], F32, name="y")
+        gated = keep.tile([P, SCALAR_PLACES], F32, name="gated")
+        by_scalar = keep.tile([P, U], F32, name="by_scalar")
+        by_vector = keep.tile([P, U], F32, name="by_vector")
+        merged = keep.tile([P, U], F32, name="merged")
 
         nc.vector.memset(w_scale[:].bitcast(I32), 0)
         nc.vector.memset(zero[:], 0.0)
-        nc.vector.memset(placed[:], 0.0)
+        nc.vector.memset(by_scalar[:], 0.0)
+        nc.vector.memset(by_vector[:], 0.0)
         nc.scalar.activation(bias[:], zero[:], GELU)
 
         x_rows = xT.rearrange("(p j) t -> p j t", j=PACK)
-        nc.sync.dma_start(planes[0], x_rows[:, 0, :])
+        nc.sync.dma_start(planes[0][:], x_rows[:, 0, :])
         nc.sync.dma_start(offs_sb[:], offs)
-        for j in (2, 1, 3):
-            nc.sync.dma_start(planes[j], x_rows[:, j, :])
-        nc.sync.dma_start(gate_sb, gate)
+        for j in range(1, PACK):
+            nc.sync.dma_start(planes[j][:], x_rows[:, j, :])
+        nc.sync.dma_start(gate_sb[:], gate)
         nc.sync.dma_start(w_codes[:].bitcast(I32), w1_words[0].rearrange("p n t -> p (n t)").bitcast(I32))
         for q in range(4):
             nc.scalar.dma_start(w_scale[32 * q : 32 * q + 4, :].bitcast(I32), w1_scales[0, 4 * q : 4 * q + 4, :].bitcast(I32))
         nc.sync.dma_start(dst_sb[:], dst)
 
-        def entries(s0, s1):
+        def picks(s0, s1):
             return offs_sb[:, s0 // STRIPE : s1 // STRIPE]
 
-        def slot(j, s0, s1):
-            return values[:, s0 * PACK : s1 * PACK].rearrange("p (s j) -> p s j", j=PACK)[:, :, j]
+        def places(s0, s1):
+            return dst_sb[:, s0 // STRIPE : s1 // STRIPE]
 
-        def round_plane(j):
-            cut = SCALAR_ROUNDS[j]
-            nc.gpsimd.tensor_copy(rounded[j][:, cut:], planes[j][:, cut:])
-            nc.scalar.copy(rounded[j][:, :cut], planes[j][:, :cut])
+        def slots(s0, s1):
+            return values[s0][:].rearrange("p (s j) -> p s j", j=PACK)
 
-        def gather_on_vector(j, s0, s1, window):
-            nc.vector.tensor_copy(slot(j, s0, s1), window.indirect(entries(s0, s1)))
+        def gather_lead(j):
+            nc.vector.tensor_copy(slots(0, LEAD)[:, :, j], planes[j][:].indirect(picks(0, LEAD)))
 
-        def gather_on_scalar(j, s0, s1):
-            nc.scalar.activation(slot(j, s0, s1), rounded[j][:].indirect(entries(s0, s1)), COPY)
+        def gather_row(j, rows, s0, s1):
+            nc.scalar.activation(rows[:, j % 2, :], planes[j][:].indirect(picks(s0, s1)), COPY)
 
-        def gather_pairs(j):
-            every_second = pairs[:, j // 2, :].rearrange("p (s e) -> p s e", e=2)[:, :, j % 2]
-            nc.vector.tensor_copy(every_second, planes[j].indirect(entries(0, PAIRED)))
+        def lay(u, rows, s0, s1):
+            pair = rows.rearrange("p e s -> p s e")
+            nc.vector.tensor_copy(slots(s0, s1)[:, :, 2 * u : 2 * u + 2], pair)
 
-        def interleave(s0, s1):
-            words = values[:, s0 * PACK : s1 * PACK].bitcast(U32).rearrange("p (c i u) -> p c u i", i=LINE, u=2)
-            nc.scalar.copy(words, pairs[:].bitcast(U32)[:, :, s0:s1].rearrange("p u (c i) -> p c u i", i=LINE))
-
-        def product(s0, s1, parts=1):
+        def product(s0, s1):
             codes = keep.tile([P, s1 - s0], U32, name=f"codes{s0}", align_bytes=64)
             scales = keep.tile([P, s1 - s0], U8, name=f"scales{s0}", align_bytes=64)
             bank = psum.tile([P, s1 - s0], F32, name=f"bank{s0}")
-            width = (s1 - s0) // parts
-            for c in range(0, s1 - s0, width):
-                part = values[:, (s0 + c) * PACK : (s0 + c + width) * PACK]
-                nc.vector.quantize_mx(out=codes[:, c : c + width].bitcast(FP8X4), scales=scales[:, c : c + width], in_=part)
+            nc.vector.quantize_mx(out=codes[:].bitcast(FP8X4), scales=scales[:], in_=values[s0][:])
             nc.tensor.matmul_mx(
                 out=bank[:],
                 lhsT=w_codes[:].bitcast(FP8X4),
@@ -108,33 +100,30 @@ def tile_picked_route2_lingelu_e_kernel(tc, xT, gate, w1_words, w1_scales, offs,
             )
             nc.scalar.activation(y[:, s0:s1], bank[:], GELU, bias=bias[:])
 
-        def scatter(s0, s1):
-            places = placed[:].indirect(dst_sb[:, s0 // STRIPE : s1 // STRIPE])
-            nc.vector.tensor_tensor(places, y[:, s0:s1], gate_sb[:, s0:s1], MULT)
+        for j in range(2):
+            gather_lead(j)
+            gather_row(j, rows01, LEAD, S)
+        for s0 in range(LEAD, S, GROUP):
+            lay(0, rows01[:, :, s0 - LEAD : s0 - LEAD + GROUP], s0, s0 + GROUP)
 
-        round_plane(0)
-        gather_on_scalar(0, PAIRED, S)
-        gather_pairs(0)
+        for j in range(2, PACK):
+            gather_lead(j)
+            for s0 in range(LEAD, S, GROUP):
+                gather_row(j, rows23[s0], s0, s0 + GROUP)
+        for s0 in range(0, S, GROUP):
+            if s0 + GROUP < S:
+                lay(1, rows23[s0 + GROUP][:], s0 + GROUP, s0 + 2 * GROUP)
+            product(s0, s0 + GROUP)
+        for s0 in range(0, SCALAR_PLACES, GROUP):
+            s1 = min(s0 + GROUP, SCALAR_PLACES)
+            nc.vector.tensor_tensor(gated[:, s0:s1], y[:, s0:s1], gate_sb[:, s0:s1], MULT)
 
-        gather_on_vector(2, PAIRED, S, planes[2])
-        gather_pairs(2)
+        nc.scalar.activation(by_scalar[:].indirect(places(0, SCALAR_PLACES)), gated[:], COPY)
+        nc.vector.tensor_tensor(by_vector[:].indirect(places(SCALAR_PLACES, S)), y[:, SCALAR_PLACES:], gate_sb[:, SCALAR_PLACES:], MULT)
 
-        round_plane(1)
-        gather_on_scalar(1, LEAD, S)
-        gather_on_scalar(1, PAIRED, LEAD)
-        gather_pairs(1)
-
-        gather_on_vector(3, LEAD, S, planes[3])
-        gather_pairs(3)
-        interleave(0, GROUP // 2)
-        interleave(GROUP // 2, GROUP)
-        interleave(GROUP, PAIRED)
-        product(LEAD, LEAD + GROUP // 2)
-        product(LEAD + GROUP // 2, S)
-        gather_on_vector(3, PAIRED, LEAD, plane3_gate[:, : T + SPARE])
-        for g in (0, 2, 1):
-            product(g * GROUP, (g + 1) * GROUP, 2 if g == 0 else 1)
-
-        scatter(LEAD, S)
-        scatter(0, LEAD)
-        nc.sync.dma_start(out, placed[:])
+        c0 = 0
+        for width in PIECES:
+            cols = slice(c0, c0 + width)
+            nc.vector.tensor_tensor(merged[:, cols], by_scalar[:, cols], by_vector[:, cols], ADD)
+            nc.sync.dma_start(out[:, cols], merged[:, cols])
+            c0 += width

@@ -18,9 +18,10 @@ P = 128
 PACK = 4
 K, T, S, N, U = 512, 1024, 512, 128, 1024
 STRIPE = 16
-GROUP = 128
-LEAD = GROUP
-SCALAR_PLACES = S // 2
+LEAD = 256
+ROWS = (256, 384, 512)
+GROUPS = (0, 128, 256, 384, 512)
+SCALAR_PLACES = (128, 320)
 PIECES = (256, 256, 256, 256)
 FLOPS = 2 * K * S * N
 
@@ -40,10 +41,12 @@ def tile_picked_route2_lingelu_e_kernel(tc, xT, gate, w1_words, w1_scales, offs,
         bias = keep.tile([P, 1], F32, name="bias")
         planes = [keep.tile([P, T], F32, name=f"plane{j}") for j in range(PACK)]
         rows01 = keep.tile([P, 2, S - LEAD], BF16, name="rows01")
-        rows23 = {s0: keep.tile([P, 2, GROUP], BF16, name=f"rows23_{s0}") for s0 in range(LEAD, S, GROUP)}
-        values = {s0: keep.tile([P, GROUP * PACK], BF16, name=f"values{s0}", align_bytes=64) for s0 in range(0, S, GROUP)}
+        stretches = list(zip(ROWS, ROWS[1:]))
+        groups = list(zip(GROUPS, GROUPS[1:]))
+        rows23 = {s0: keep.tile([P, 2, s1 - s0], BF16, name=f"rows23_{s0}") for s0, s1 in stretches}
+        values = keep.tile([P, S * PACK], BF16, name="values", align_bytes=64)
         y = keep.tile([P, S], F32, name="y")
-        gated = keep.tile([P, SCALAR_PLACES], F32, name="gated")
+        gated = keep.tile([P, SCALAR_PLACES[1] - SCALAR_PLACES[0]], F32, name="gated")
         by_scalar = keep.tile([P, U], F32, name="by_scalar")
         by_vector = keep.tile([P, U], F32, name="by_vector")
         merged = keep.tile([P, U], F32, name="merged")
@@ -72,23 +75,23 @@ def tile_picked_route2_lingelu_e_kernel(tc, xT, gate, w1_words, w1_scales, offs,
             return dst_sb[:, s0 // STRIPE : s1 // STRIPE]
 
         def slots(s0, s1):
-            return values[s0][:].rearrange("p (s j) -> p s j", j=PACK)
+            return values[:, s0 * PACK : s1 * PACK].rearrange("p (s j) -> p s j", j=PACK)
 
-        def gather_lead(j):
-            nc.vector.tensor_copy(slots(0, LEAD)[:, :, j], planes[j][:].indirect(picks(0, LEAD)))
+        def gather_lead(j, s0, s1):
+            nc.vector.tensor_copy(slots(s0, s1)[:, :, j], planes[j][:].indirect(picks(s0, s1)))
 
         def gather_row(j, rows, s0, s1):
             nc.scalar.activation(rows[:, j % 2, :], planes[j][:].indirect(picks(s0, s1)), COPY)
 
-        def lay(u, rows, s0, s1):
+        def lay(u, rows, s0, s1, copy):
             pair = rows.rearrange("p e s -> p s e")
-            nc.vector.tensor_copy(slots(s0, s1)[:, :, 2 * u : 2 * u + 2], pair)
+            copy(slots(s0, s1)[:, :, 2 * u : 2 * u + 2], pair)
 
         def product(s0, s1):
             codes = keep.tile([P, s1 - s0], U32, name=f"codes{s0}", align_bytes=64)
             scales = keep.tile([P, s1 - s0], U8, name=f"scales{s0}", align_bytes=64)
             bank = psum.tile([P, s1 - s0], F32, name=f"bank{s0}")
-            nc.vector.quantize_mx(out=codes[:].bitcast(FP8X4), scales=scales[:], in_=values[s0][:])
+            nc.vector.quantize_mx(out=codes[:].bitcast(FP8X4), scales=scales[:], in_=values[:, s0 * PACK : s1 * PACK])
             nc.tensor.matmul_mx(
                 out=bank[:],
                 lhsT=w_codes[:].bitcast(FP8X4),
@@ -101,25 +104,31 @@ def tile_picked_route2_lingelu_e_kernel(tc, xT, gate, w1_words, w1_scales, offs,
             nc.scalar.activation(y[:, s0:s1], bank[:], GELU, bias=bias[:])
 
         for j in range(2):
-            gather_lead(j)
+            gather_lead(j, 0, LEAD)
             gather_row(j, rows01, LEAD, S)
-        for s0 in range(LEAD, S, GROUP):
-            lay(0, rows01[:, :, s0 - LEAD : s0 - LEAD + GROUP], s0, s0 + GROUP)
-
+        lay(0, rows01[:], LEAD, S, nc.scalar.copy)
+        gather_lead(2, 0, LEAD)
         for j in range(2, PACK):
-            gather_lead(j)
-            for s0 in range(LEAD, S, GROUP):
-                gather_row(j, rows23[s0], s0, s0 + GROUP)
-        for s0 in range(0, S, GROUP):
-            if s0 + GROUP < S:
-                lay(1, rows23[s0 + GROUP][:], s0 + GROUP, s0 + 2 * GROUP)
-            product(s0, s0 + GROUP)
-        for s0 in range(0, SCALAR_PLACES, GROUP):
-            s1 = min(s0 + GROUP, SCALAR_PLACES)
-            nc.vector.tensor_tensor(gated[:, s0:s1], y[:, s0:s1], gate_sb[:, s0:s1], MULT)
+            for s0, s1 in stretches:
+                gather_row(j, rows23[s0], s0, s1)
+        for s0, s1 in groups[:2]:
+            gather_lead(3, s0, s1)
+        third, last = stretches
+        lay(1, rows23[third[0]][:], *third, nc.scalar.copy)
+        for s0, s1 in groups[:2]:
+            product(s0, s1)
+        lay(1, rows23[last[0]][:], *last, nc.vector.tensor_copy)
+        for s0, s1 in groups[2:]:
+            product(s0, s1)
 
-        nc.scalar.activation(by_scalar[:].indirect(places(0, SCALAR_PLACES)), gated[:], COPY)
-        nc.vector.tensor_tensor(by_vector[:].indirect(places(SCALAR_PLACES, S)), y[:, SCALAR_PLACES:], gate_sb[:, SCALAR_PLACES:], MULT)
+        def scatter_on_vector(s0, s1):
+            nc.vector.tensor_tensor(by_vector[:].indirect(places(s0, s1)), y[:, s0:s1], gate_sb[:, s0:s1], MULT)
+
+        s0, s1 = SCALAR_PLACES
+        scatter_on_vector(0, s0)
+        nc.vector.tensor_tensor(gated[:], y[:, s0:s1], gate_sb[:, s0:s1], MULT)
+        nc.scalar.activation(by_scalar[:].indirect(places(s0, s1)), gated[:], COPY)
+        scatter_on_vector(s1, S)
 
         c0 = 0
         for width in PIECES:

@@ -20,7 +20,7 @@ K, T, S, N, U = 512, 1024, 512, 128, 1024
 STRIPE = 16
 LEAD = 256
 ROWS = (256, 384, 512)
-GROUPS = (0, 128, 256, 384, 512)
+GROUPS = (0, 64, 128, 256, 384, 512)
 SCALAR_PLACES = (128, 320)
 PIECES = (256, 256, 256, 256)
 FLOPS = 2 * K * S * N
@@ -106,19 +106,20 @@ def tile_picked_route2_lingelu_e_kernel(tc, xT, gate, w1_words, w1_scales, offs,
         for j in range(2):
             gather_lead(j, 0, LEAD)
             gather_row(j, rows01, LEAD, S)
-        lay(0, rows01[:], LEAD, S, nc.scalar.copy)
+        for (s0, s1), copy in zip(stretches, (nc.vector.tensor_copy, nc.scalar.copy)):
+            lay(0, rows01[:, :, s0 - LEAD : s1 - LEAD], s0, s1, copy)
         gather_lead(2, 0, LEAD)
         for j in range(2, PACK):
             for s0, s1 in stretches:
                 gather_row(j, rows23[s0], s0, s1)
-        for s0, s1 in groups[:2]:
-            gather_lead(3, s0, s1)
+        for s0 in range(0, LEAD, LEAD // 2):
+            gather_lead(3, s0, s0 + LEAD // 2)
         third, last = stretches
         lay(1, rows23[third[0]][:], *third, nc.scalar.copy)
-        for s0, s1 in groups[:2]:
+        for s0, s1 in groups[:3]:
             product(s0, s1)
         lay(1, rows23[last[0]][:], *last, nc.vector.tensor_copy)
-        for s0, s1 in groups[2:]:
+        for s0, s1 in groups[3:]:
             product(s0, s1)
 
         def scatter_on_vector(s0, s1):

@@ -20,9 +20,9 @@ K, T, S, N, U = 512, 1024, 512, 128, 1024
 STRIPE = 16
 LEAD = 256
 ROWS = (256, 384, 512)
-GROUPS = (0, 64, 128, 256, 384, 512)
+GROUPS = (0, 64, 128, 256, 320, 448, 512)
 SCALAR_PLACES = (128, 320)
-PIECES = (256, 256, 256, 256)
+PIECES = (192, 256, 256, 320)
 FLOPS = 2 * K * S * N
 
 
@@ -116,10 +116,10 @@ def tile_picked_route2_lingelu_e_kernel(tc, xT, gate, w1_words, w1_scales, offs,
             gather_lead(3, s0, s0 + LEAD // 2)
         third, last = stretches
         lay(1, rows23[third[0]][:], *third, nc.scalar.copy)
-        for s0, s1 in groups[:3]:
+        for s0, s1 in groups[:2]:
             product(s0, s1)
         lay(1, rows23[last[0]][:], *last, nc.vector.tensor_copy)
-        for s0, s1 in groups[3:]:
+        for s0, s1 in groups[2:]:
             product(s0, s1)
 
         def scatter_on_vector(s0, s1):

@@ -18,9 +18,13 @@ P = 128
 PACK = 4
 K, T, S, N, U = 512, 1024, 512, 128, 1024
 STRIPE = 16
-LEAD = 256
-ROWS = (256, 384, 512)
-GROUPS = (0, 64, 128, 256, 320, 448, 512)
+HALF = 256
+LEAD = (0, 128)
+NEXT = (128, 256)
+EARLY = (256, 320)
+LAST = (320, 416)
+FILL = (416, 512)
+GROUPS = ((0, 64), (64, 128), (256, 320), (128, 256), (448, 512), (320, 448))
 SCALAR_PLACES = (128, 320)
 PIECES = (192, 256, 256, 320)
 FLOPS = 2 * K * S * N
@@ -40,10 +44,8 @@ def tile_picked_route2_lingelu_e_kernel(tc, xT, gate, w1_words, w1_scales, offs,
         zero = keep.tile([P, 1], F32, name="zero")
         bias = keep.tile([P, 1], F32, name="bias")
         planes = [keep.tile([P, T], F32, name=f"plane{j}") for j in range(PACK)]
-        rows01 = keep.tile([P, 2, S - LEAD], BF16, name="rows01")
-        stretches = list(zip(ROWS, ROWS[1:]))
-        groups = list(zip(GROUPS, GROUPS[1:]))
-        rows23 = {s0: keep.tile([P, 2, s1 - s0], BF16, name=f"rows23_{s0}") for s0, s1 in stretches}
+        rows01 = keep.tile([P, 2, S - HALF], BF16, name="rows01")
+        rows23 = {s0: keep.tile([P, 2, s1 - s0], BF16, name=f"rows23_{s0}") for s0, s1 in (EARLY, NEXT, FILL, LAST)}
         values = keep.tile([P, S * PACK], BF16, name="values", align_bytes=64)
         y = keep.tile([P, S], F32, name="y")
         gated = keep.tile([P, SCALAR_PLACES[1] - SCALAR_PLACES[0]], F32, name="gated")
@@ -104,32 +106,33 @@ def tile_picked_route2_lingelu_e_kernel(tc, xT, gate, w1_words, w1_scales, offs,
             nc.scalar.activation(y[:, s0:s1], bank[:], GELU, bias=bias[:])
 
         for j in range(2):
-            gather_lead(j, 0, LEAD)
-            gather_row(j, rows01, LEAD, S)
-        for (s0, s1), copy in zip(stretches, (nc.vector.tensor_copy, nc.scalar.copy)):
-            lay(0, rows01[:, :, s0 - LEAD : s1 - LEAD], s0, s1, copy)
-        gather_lead(2, 0, LEAD)
+            gather_lead(j, 0, HALF)
+            gather_row(j, rows01, HALF, S)
+        middle = (HALF + S) // 2
+        for (s0, s1), copy in (((HALF, middle), nc.vector.tensor_copy), ((middle, S), nc.scalar.copy)):
+            lay(0, rows01[:, :, s0 - HALF : s1 - HALF], s0, s1, copy)
         for j in range(2, PACK):
-            for s0, s1 in stretches:
+            gather_lead(j, *LEAD)
+            nc.vector.tensor_copy(rows23[FILL[0]][:, j % 2, :], planes[j][:].indirect(picks(*FILL)))
+            for s0, s1 in (EARLY, NEXT, LAST):
                 gather_row(j, rows23[s0], s0, s1)
-        for s0 in range(0, LEAD, LEAD // 2):
-            gather_lead(3, s0, s0 + LEAD // 2)
-        third, last = stretches
-        lay(1, rows23[third[0]][:], *third, nc.scalar.copy)
-        for s0, s1 in groups[:2]:
+        for s0, s1 in (EARLY, LAST):
+            lay(1, rows23[s0][:], s0, s1, nc.scalar.copy)
+        for s0, s1 in GROUPS[:2]:
             product(s0, s1)
-        lay(1, rows23[last[0]][:], *last, nc.vector.tensor_copy)
-        for s0, s1 in groups[2:]:
+        for s0, s1 in (NEXT, FILL):
+            lay(1, rows23[s0][:], s0, s1, nc.vector.tensor_copy)
+        for s0, s1 in GROUPS[2:]:
             product(s0, s1)
 
-        def scatter_on_vector(s0, s1):
-            nc.vector.tensor_tensor(by_vector[:].indirect(places(s0, s1)), y[:, s0:s1], gate_sb[:, s0:s1], MULT)
+        def scatter_on_vector(window, s0, s1):
+            nc.vector.tensor_tensor(window[:].indirect(places(s0, s1)), y[:, s0:s1], gate_sb[:, s0:s1], MULT)
 
         s0, s1 = SCALAR_PLACES
-        scatter_on_vector(0, s0)
+        scatter_on_vector(by_vector, 0, s0)
         nc.vector.tensor_tensor(gated[:], y[:, s0:s1], gate_sb[:, s0:s1], MULT)
         nc.scalar.activation(by_scalar[:].indirect(places(s0, s1)), gated[:], COPY)
-        scatter_on_vector(s1, S)
+        scatter_on_vector(by_vector, s1, S)
 
         c0 = 0
         for width in PIECES:

@@ -24,7 +24,9 @@ NEXT = (128, 256)
 EARLY = (256, 320)
 LAST = (320, 416)
 FILL = (416, 512)
-GROUPS = ((0, 64), (64, 128), (256, 320), (128, 256), (448, 512), (320, 448))
+LAID_BY_SCALAR = (EARLY, (320, 384))
+LAID_BY_VECTOR = (NEXT, (384, 512))
+GROUPS = ((0, 64), (64, 128), (256, 320), (128, 256), (320, 384), (384, 512))
 SCALAR_PLACES = (128, 320)
 PIECES = (192, 256, 256, 320)
 FLOPS = 2 * K * S * N
@@ -45,7 +47,7 @@ def tile_picked_route2_lingelu_e_kernel(tc, xT, gate, w1_words, w1_scales, offs,
         bias = keep.tile([P, 1], F32, name="bias")
         planes = [keep.tile([P, T], F32, name=f"plane{j}") for j in range(PACK)]
         rows01 = keep.tile([P, 2, S - HALF], BF16, name="rows01")
-        rows23 = {s0: keep.tile([P, 2, s1 - s0], BF16, name=f"rows23_{s0}") for s0, s1 in (EARLY, NEXT, FILL, LAST)}
+        rows23 = keep.tile([P, 2, S - LEAD[1]], BF16, name="rows23")
         values = keep.tile([P, S * PACK], BF16, name="values", align_bytes=64)
         y = keep.tile([P, S], F32, name="y")
         gated = keep.tile([P, SCALAR_PLACES[1] - SCALAR_PLACES[0]], F32, name="gated")
@@ -64,11 +66,11 @@ def tile_picked_route2_lingelu_e_kernel(tc, xT, gate, w1_words, w1_scales, offs,
         nc.sync.dma_start(offs_sb[:], offs)
         for j in range(1, PACK):
             nc.sync.dma_start(planes[j][:], x_rows[:, j, :])
-        nc.sync.dma_start(gate_sb[:], gate)
         nc.sync.dma_start(w_codes[:].bitcast(I32), w1_words[0].rearrange("p n t -> p (n t)").bitcast(I32))
         for q in range(4):
             nc.scalar.dma_start(w_scale[32 * q : 32 * q + 4, :].bitcast(I32), w1_scales[0, 4 * q : 4 * q + 4, :].bitcast(I32))
         nc.sync.dma_start(dst_sb[:], dst)
+        nc.sync.dma_start(gate_sb[:], gate)
 
         def picks(s0, s1):
             return offs_sb[:, s0 // STRIPE : s1 // STRIPE]
@@ -111,17 +113,20 @@ def tile_picked_route2_lingelu_e_kernel(tc, xT, gate, w1_words, w1_scales, offs,
         middle = (HALF + S) // 2
         for (s0, s1), copy in (((HALF, middle), nc.vector.tensor_copy), ((middle, S), nc.scalar.copy)):
             lay(0, rows01[:, :, s0 - HALF : s1 - HALF], s0, s1, copy)
-        for j in range(2, PACK):
+        def stretch(s0, s1):
+            return rows23[:, :, s0 - LEAD[1] : s1 - LEAD[1]]
+
+        for j, stretches in ((2, ((NEXT[0], LAST[1]),)), (3, (EARLY, NEXT, LAST))):
             gather_lead(j, *LEAD)
-            nc.vector.tensor_copy(rows23[FILL[0]][:, j % 2, :], planes[j][:].indirect(picks(*FILL)))
-            for s0, s1 in (EARLY, NEXT, LAST):
-                gather_row(j, rows23[s0], s0, s1)
-        for s0, s1 in (EARLY, LAST):
-            lay(1, rows23[s0][:], s0, s1, nc.scalar.copy)
+            nc.vector.tensor_copy(stretch(*FILL)[:, j % 2, :], planes[j][:].indirect(picks(*FILL)))
+            for s0, s1 in stretches:
+                gather_row(j, stretch(s0, s1), s0, s1)
+        for s0, s1 in LAID_BY_SCALAR:
+            lay(1, stretch(s0, s1), s0, s1, nc.scalar.copy)
         for s0, s1 in GROUPS[:2]:
             product(s0, s1)
-        for s0, s1 in (NEXT, FILL):
-            lay(1, rows23[s0][:], s0, s1, nc.vector.tensor_copy)
+        for s0, s1 in LAID_BY_VECTOR:
+            lay(1, stretch(s0, s1), s0, s1, nc.vector.tensor_copy)
         for s0, s1 in GROUPS[2:]:
             product(s0, s1)
 

@@ -18,16 +18,13 @@ P = 128
 PACK = 4
 K, T, S, N, U = 512, 1024, 512, 128, 1024
 STRIPE = 16
-HALF = 256
-LEAD = (0, 128)
-NEXT = (128, 256)
-EARLY = (256, 320)
-LAST = (320, 416)
-FILL = (416, 512)
-LAID_BY_SCALAR = (EARLY, (320, 384))
-LAID_BY_VECTOR = (NEXT, (384, 512))
-GROUPS = ((0, 64), (64, 128), (256, 320), (128, 256), (320, 384), (384, 512))
-SCALAR_PLACES = (128, 320)
+ROW_ALIGN = 256
+LOAD_ORDER = (2, 0, 1, 3)
+SPLIT01 = 288
+VECTOR23 = (128, 320)
+SCALAR3 = ((0, 64), (64, 128), (320, 448), (448, 512))
+GROUPS = ((0, 64), (64, 128), (128, 256), (256, 320), (320, 448), (448, 512))
+GATED = ((0, 128), (128, 256))
 PIECES = (192, 256, 256, 320)
 FLOPS = 2 * K * S * N
 
@@ -42,18 +39,16 @@ def tile_picked_route2_lingelu_e_kernel(tc, xT, gate, w1_words, w1_scales, offs,
         dst_sb = keep.tile([P, S // STRIPE], U16, name="dst_sb")
         w_codes = keep.tile([P, N], U32, name="w_codes", align_bytes=64)
         w_scale = keep.tile([P, N], U8, name="w_scale", align_bytes=64)
-        gate_sb = keep.tile([P, S], F32, name="gate_sb")
+        gate_sb = keep.tile([P, S], F32, name="gate_sb", align_bytes=ROW_ALIGN)
         zero = keep.tile([P, 1], F32, name="zero")
         bias = keep.tile([P, 1], F32, name="bias")
-        planes = [keep.tile([P, T], F32, name=f"plane{j}") for j in range(PACK)]
-        rows01 = keep.tile([P, 2, S - HALF], BF16, name="rows01")
-        rows23 = keep.tile([P, 2, S - LEAD[1]], BF16, name="rows23")
+        planes = [keep.tile([P, T], F32, name=f"plane{j}", align_bytes=ROW_ALIGN) for j in range(PACK)]
         values = keep.tile([P, S * PACK], BF16, name="values", align_bytes=64)
         y = keep.tile([P, S], F32, name="y")
-        gated = keep.tile([P, SCALAR_PLACES[1] - SCALAR_PLACES[0]], F32, name="gated")
+        gated = keep.tile([P, GATED[-1][1]], F32, name="gated")
         by_scalar = keep.tile([P, U], F32, name="by_scalar")
         by_vector = keep.tile([P, U], F32, name="by_vector")
-        merged = keep.tile([P, U], F32, name="merged")
+        merged = keep.tile([P, U], F32, name="merged", align_bytes=ROW_ALIGN)
 
         nc.vector.memset(w_scale[:].bitcast(I32), 0)
         nc.vector.memset(zero[:], 0.0)
@@ -62,9 +57,9 @@ def tile_picked_route2_lingelu_e_kernel(tc, xT, gate, w1_words, w1_scales, offs,
         nc.scalar.activation(bias[:], zero[:], GELU)
 
         x_rows = xT.rearrange("(p j) t -> p j t", j=PACK)
-        nc.sync.dma_start(planes[0][:], x_rows[:, 0, :])
+        nc.sync.dma_start(planes[LOAD_ORDER[0]][:], x_rows[:, LOAD_ORDER[0], :])
         nc.sync.dma_start(offs_sb[:], offs)
-        for j in range(1, PACK):
+        for j in LOAD_ORDER[1:]:
             nc.sync.dma_start(planes[j][:], x_rows[:, j, :])
         nc.sync.dma_start(w_codes[:].bitcast(I32), w1_words[0].rearrange("p n t -> p (n t)").bitcast(I32))
         for q in range(4):
@@ -72,24 +67,20 @@ def tile_picked_route2_lingelu_e_kernel(tc, xT, gate, w1_words, w1_scales, offs,
         nc.sync.dma_start(dst_sb[:], dst)
         nc.sync.dma_start(gate_sb[:], gate)
 
-        def picks(s0, s1):
-            return offs_sb[:, s0 // STRIPE : s1 // STRIPE]
+        def window(j, s0, s1):
+            return planes[j][:].indirect(offs_sb[:, s0 // STRIPE : s1 // STRIPE])
 
         def places(s0, s1):
             return dst_sb[:, s0 // STRIPE : s1 // STRIPE]
 
-        def slots(s0, s1):
-            return values[:, s0 * PACK : s1 * PACK].rearrange("p (s j) -> p s j", j=PACK)
+        def slot(j, s0, s1):
+            return values[:, s0 * PACK + j : s1 * PACK : PACK]
 
-        def gather_lead(j, s0, s1):
-            nc.vector.tensor_copy(slots(s0, s1)[:, :, j], planes[j][:].indirect(picks(s0, s1)))
+        def gather_on_vector(j, s0, s1):
+            nc.vector.tensor_copy(slot(j, s0, s1), window(j, s0, s1))
 
-        def gather_row(j, rows, s0, s1):
-            nc.scalar.activation(rows[:, j % 2, :], planes[j][:].indirect(picks(s0, s1)), COPY)
-
-        def lay(u, rows, s0, s1, copy):
-            pair = rows.rearrange("p e s -> p s e")
-            copy(slots(s0, s1)[:, :, 2 * u : 2 * u + 2], pair)
+        def gather_on_scalar(j, s0, s1):
+            nc.scalar.activation(slot(j, s0, s1), window(j, s0, s1), COPY)
 
         def product(s0, s1):
             codes = keep.tile([P, s1 - s0], U32, name=f"codes{s0}", align_bytes=64)
@@ -107,37 +98,23 @@ def tile_picked_route2_lingelu_e_kernel(tc, xT, gate, w1_words, w1_scales, offs,
             )
             nc.scalar.activation(y[:, s0:s1], bank[:], GELU, bias=bias[:])
 
+        gather_on_vector(2, *VECTOR23)
+        gather_on_scalar(2, 0, VECTOR23[0])
+        gather_on_scalar(2, VECTOR23[1], S)
         for j in range(2):
-            gather_lead(j, 0, HALF)
-            gather_row(j, rows01, HALF, S)
-        middle = (HALF + S) // 2
-        for (s0, s1), copy in (((HALF, middle), nc.vector.tensor_copy), ((middle, S), nc.scalar.copy)):
-            lay(0, rows01[:, :, s0 - HALF : s1 - HALF], s0, s1, copy)
-        def stretch(s0, s1):
-            return rows23[:, :, s0 - LEAD[1] : s1 - LEAD[1]]
-
-        for j, stretches in ((2, ((NEXT[0], LAST[1]),)), (3, (EARLY, NEXT, LAST))):
-            gather_lead(j, *LEAD)
-            nc.vector.tensor_copy(stretch(*FILL)[:, j % 2, :], planes[j][:].indirect(picks(*FILL)))
-            for s0, s1 in stretches:
-                gather_row(j, stretch(s0, s1), s0, s1)
-        for s0, s1 in LAID_BY_SCALAR:
-            lay(1, stretch(s0, s1), s0, s1, nc.scalar.copy)
-        for s0, s1 in GROUPS[:2]:
-            product(s0, s1)
-        for s0, s1 in LAID_BY_VECTOR:
-            lay(1, stretch(s0, s1), s0, s1, nc.vector.tensor_copy)
-        for s0, s1 in GROUPS[2:]:
+            gather_on_vector(j, 0, SPLIT01)
+            gather_on_scalar(j, SPLIT01, S)
+        gather_on_vector(3, *VECTOR23)
+        for s0, s1 in SCALAR3:
+            gather_on_scalar(3, s0, s1)
+        for s0, s1 in GROUPS:
             product(s0, s1)
 
-        def scatter_on_vector(window, s0, s1):
-            nc.vector.tensor_tensor(window[:].indirect(places(s0, s1)), y[:, s0:s1], gate_sb[:, s0:s1], MULT)
-
-        s0, s1 = SCALAR_PLACES
-        scatter_on_vector(by_vector, 0, s0)
-        nc.vector.tensor_tensor(gated[:], y[:, s0:s1], gate_sb[:, s0:s1], MULT)
-        nc.scalar.activation(by_scalar[:].indirect(places(s0, s1)), gated[:], COPY)
-        scatter_on_vector(by_vector, s1, S)
+        for s0, s1 in GATED:
+            nc.vector.tensor_tensor(gated[:, s0:s1], y[:, s0:s1], gate_sb[:, s0:s1], MULT)
+        share = GATED[-1][1]
+        nc.scalar.activation(by_scalar[:].indirect(places(0, share)), gated[:], COPY)
+        nc.vector.tensor_tensor(by_vector[:].indirect(places(share, S)), y[:, share:S], gate_sb[:, share:S], MULT)
 
         c0 = 0
         for width in PIECES:

@@ -20,7 +20,7 @@ K, T, S, N, U = 512, 1024, 512, 128, 1024
 STRIPE = 16
 ROW_ALIGN = 256
 LOAD_ORDER = (2, 0, 1, 3)
-SPLIT01 = 288
+SPLIT01 = 256
 VECTOR23 = (128, 320)
 SCALAR3 = ((0, 64), (64, 128), (320, 448), (448, 512))
 GROUPS = ((0, 64), (64, 128), (128, 256), (256, 320), (320, 448), (448, 512))

from contextlib import ExitStack

import concourse.mybir as mybir

F32 = mybir.dt.float32
BF16 = mybir.dt.bfloat16
I32 = mybir.dt.int32
U32 = mybir.dt.uint32
U16 = mybir.dt.uint16
U8 = mybir.dt.uint8
FP8X4 = mybir.dt.float8_e4m3fn_x4
GELU = mybir.ActivationFunctionType.Gelu_apprx_tanh
COPY = mybir.ActivationFunctionType.Copy
MULT = mybir.AluOpType.mult
ADD = mybir.AluOpType.add

P = 128
PACK = 4
K, T, S, N, U = 512, 1024, 512, 128, 1024
STRIPE = 16
ROW_ALIGN = 256
LOAD_ORDER = (2, 0, 1, 3)
SPLIT01 = 256
VECTOR23 = (128, 320)
SCALAR3 = ((0, 64), (64, 128), (320, 448), (448, 512))
GROUPS = ((0, 64), (64, 128), (128, 256), (256, 320), (320, 448), (448, 512))
GATED = ((0, 128), (128, 256))
PIECES = (192, 256, 256, 320)
FLOPS = 2 * K * S * N


def tile_picked_route2_lingelu_e_kernel(tc, xT, gate, w1_words, w1_scales, offs, dst, out):
    nc = tc.nc
    with ExitStack() as ctx:
        keep = ctx.enter_context(tc.tile_pool(name="keep", bufs=1))
        psum = ctx.enter_context(tc.psum_pool(name="psum", bufs=1))

        offs_sb = keep.tile([P, S // STRIPE], U16, name="offs_sb")
        dst_sb = keep.tile([P, S // STRIPE], U16, name="dst_sb")
        w_codes = keep.tile([P, N], U32, name="w_codes", align_bytes=64)
        w_scale = keep.tile([P, N], U8, name="w_scale", align_bytes=64)
        gate_sb = keep.tile([P, S], F32, name="gate_sb", align_bytes=ROW_ALIGN)
        zero = keep.tile([P, 1], F32, name="zero")
        bias = keep.tile([P, 1], F32, name="bias")
        planes = [keep.tile([P, T], F32, name=f"plane{j}", align_bytes=ROW_ALIGN) for j in range(PACK)]
        values = keep.tile([P, S * PACK], BF16, name="values", align_bytes=64)
        y = keep.tile([P, S], F32, name="y")
        gated = keep.tile([P, GATED[-1][1]], F32, name="gated")
        by_scalar = keep.tile([P, U], F32, name="by_scalar")
        by_vector = keep.tile([P, U], F32, name="by_vector")
        merged = keep.tile([P, U], F32, name="merged", align_bytes=ROW_ALIGN)

        nc.vector.memset(w_scale[:].bitcast(I32), 0)
        nc.vector.memset(zero[:], 0.0)
        nc.vector.memset(by_scalar[:], 0.0)
        nc.vector.memset(by_vector[:], 0.0)
        nc.scalar.activation(bias[:], zero[:], GELU)

        x_rows = xT.rearrange("(p j) t -> p j t", j=PACK)
        nc.sync.dma_start(planes[LOAD_ORDER[0]][:], x_rows[:, LOAD_ORDER[0], :])
        nc.sync.dma_start(offs_sb[:], offs)
        for j in LOAD_ORDER[1:]:
            nc.sync.dma_start(planes[j][:], x_rows[:, j, :])
        nc.sync.dma_start(w_codes[:].bitcast(I32), w1_words[0].rearrange("p n t -> p (n t)").bitcast(I32))
        for q in range(4):
            nc.scalar.dma_start(w_scale[32 * q : 32 * q + 4, :].bitcast(I32), w1_scales[0, 4 * q : 4 * q + 4, :].bitcast(I32))
        nc.sync.dma_start(dst_sb[:], dst)
        nc.sync.dma_start(gate_sb[:], gate)

        def window(j, s0, s1):
            return planes[j][:].indirect(offs_sb[:, s0 // STRIPE : s1 // STRIPE])

        def places(s0, s1):
            return dst_sb[:, s0 // STRIPE : s1 // STRIPE]

        def slot(j, s0, s1):
            return values[:, s0 * PACK + j : s1 * PACK : PACK]

        def gather_on_vector(j, s0, s1):
            nc.vector.tensor_copy(slot(j, s0, s1), window(j, s0, s1))

        def gather_on_scalar(j, s0, s1):
            nc.scalar.activation(slot(j, s0, s1), window(j, s0, s1), COPY)

        def product(s0, s1):
            codes = keep.tile([P, s1 - s0], U32, name=f"codes{s0}", align_bytes=64)
            scales = keep.tile([P, s1 - s0], U8, name=f"scales{s0}", align_bytes=64)
            bank = psum.tile([P, s1 - s0], F32, name=f"bank{s0}")
            nc.vector.quantize_mx(out=codes[:].bitcast(FP8X4), scales=scales[:], in_=values[:, s0 * PACK : s1 * PACK])
            nc.tensor.matmul_mx(
                out=bank[:],
                lhsT=w_codes[:].bitcast(FP8X4),
                lhsT_scale=w_scale[:],
                rhs=codes[:].bitcast(FP8X4),
                rhs_scale=scales[:],
                start=True,
                stop=True,
            )
            nc.scalar.activation(y[:, s0:s1], bank[:], GELU, bias=bias[:])

        gather_on_vector(2, *VECTOR23)
        gather_on_scalar(2, 0, VECTOR23[0])
        gather_on_scalar(2, VECTOR23[1], S)
        for j in range(2):
            gather_on_vector(j, 0, SPLIT01)
            gather_on_scalar(j, SPLIT01, S)
        gather_on_vector(3, *VECTOR23)
        for s0, s1 in SCALAR3:
            gather_on_scalar(3, s0, s1)
        for s0, s1 in GROUPS:
            product(s0, s1)

        for s0, s1 in GATED:
            nc.vector.tensor_tensor(gated[:, s0:s1], y[:, s0:s1], gate_sb[:, s0:s1], MULT)
        share = GATED[-1][1]
        nc.scalar.activation(by_scalar[:].indirect(places(0, share)), gated[:], COPY)
        nc.vector.tensor_tensor(by_vector[:].indirect(places(share, S)), y[:, share:S], gate_sb[:, share:S], MULT)

        c0 = 0
        for width in PIECES:
            cols = slice(c0, c0 + width)
            nc.vector.tensor_tensor(merged[:, cols], by_scalar[:, cols], by_vector[:, cols], ADD)
            nc.sync.dma_start(out[:, cols], merged[:, cols])
            c0 += width
